import numpy as np
import ml_dtypes


def mxq(x, axis, fmt="e4m3"):
    dtype, down = {"e4m3": (ml_dtypes.float8_e4m3fn, 7), "e5m2": (ml_dtypes.float8_e5m2, 14)}[fmt]
    v = np.moveaxis(np.asarray(x, np.float32).astype(ml_dtypes.bfloat16).astype(np.float64), axis, -1)
    blocks = v.reshape(v.shape[:-1] + (-1, 32))
    amax = np.abs(blocks).max(-1, keepdims=True)
    byte = np.maximum(np.where(amax > 0, np.frexp(amax)[1] - 1 + 127, 0) - down, 1)
    scale = np.exp2(byte - 127.0)
    codes = (blocks / scale).astype(np.float32).astype(dtype).astype(np.float64)
    return np.moveaxis((codes * scale).reshape(v.shape), -1, axis)


WIDE = False


def mx_kscale(k):
    if not WIDE:
        return np.ones(k)
    levels = np.array([10, -10, 5, -5, 0])
    if k % 512:
        return np.exp2(np.random.permutation(np.resize(levels, k // 32))).repeat(32)
    a = np.empty((k // 512, 16))
    for p in range(k // 512):
        a[p, :8] = np.random.permutation(np.resize(levels, 8))
        for g in range(8):
            far = levels[np.abs(levels - a[p, g]) >= 10]
            a[p, g + 8] = far[np.random.randint(len(far))]
    return np.exp2(a.ravel()).repeat(32)


def f64(x):
    return np.asarray(x).astype(np.float64)


def striped(idx):
    return np.tile(idx.reshape(-1, 16).T, (8, 1)).astype(np.uint16)


def unstriped(offs):
    return offs[:16].T.reshape(-1).astype(np.int64)


E2M1 = np.array([0.0, 0.5, 1.0, 1.5, 2.0, 3.0, 4.0, 6.0, -0.0, -0.5, -1.0, -1.5, -2.0, -3.0, -4.0, -6.0])


def pack_weight(w, fmt):
    k, n = w.shape
    w = f64(np.asarray(w, np.float32).astype(ml_dtypes.bfloat16)).reshape(k // 32, 32, n)
    amax = np.abs(w).max(1)
    if fmt == "e4m3":
        byte = np.frexp(amax)[1] - 1 + 127 - 7
    else:
        mant, ex = np.frexp(amax / 6.0)
        byte = np.where(mant > 0.5, ex, ex - 1) + 127
    byte = np.clip(np.where(amax > 0, byte, 1), 1, 254)
    scaled = (w * np.exp2(127.0 - byte)[:, None, :]).reshape(k, n).astype(np.float32)
    by_word = np.ascontiguousarray(scaled.reshape(k // 512, 128, 4, n).transpose(0, 1, 3, 2))
    if fmt == "e4m3":
        words = by_word.astype(ml_dtypes.float8_e4m3fn).view(np.uint8)
    else:
        c = by_word.astype(ml_dtypes.float4_e2m1fn).view(np.uint8) & 0xF
        words = (c[..., 0::2] | (c[..., 1::2] << 4)).reshape(k // 512, 128, 2 * n)
    return np.ascontiguousarray(words), np.ascontiguousarray(byte.astype(np.uint8).reshape(k // 512, 16, n))


def unpack_weight(words, scales, fmt):
    g, _, n = scales.shape
    words = np.ascontiguousarray(words).reshape(g, 128, n, -1)
    if fmt == "e4m3":
        vals = words.view(ml_dtypes.float8_e4m3fn).astype(np.float64)
    else:
        nib = np.empty((g, 128, n, 4), np.uint8)
        nib[..., 0::2] = words & 0xF
        nib[..., 1::2] = words >> 4
        vals = E2M1[nib]
    vals = vals * np.repeat(np.exp2(scales.astype(np.float64) - 127.0), 8, axis=1)[..., None]
    return vals.transpose(0, 1, 3, 2).reshape(g * 512, n)


def pack_table(v):
    words, scales = pack_weight(v, "e4m3")
    return np.concatenate([words.reshape(words.shape[0], -1), scales.reshape(scales.shape[0], -1)], axis=1)


def unpack_table(tab):
    g, t = tab.shape[0], tab.shape[1] // 528
    return unpack_weight(tab[:, :512 * t].reshape(g, 128, t, 4), tab[:, 512 * t:].reshape(g, 16, t), "e4m3")


def gelu(v):
    return 0.5 * v * (1.0 + np.tanh(np.sqrt(2.0 / np.pi) * (v + 0.044715 * v**3)))


K, M, T, S = 1024, 512, 2048, 256


def setup_inputs():
    n = np.random.standard_normal
    s = mx_kscale(K)[:, None]
    p_w0 = pack_weight(n((K, M)) / np.sqrt(3 * K) / s, "e2m1")
    p_w1 = pack_weight(n((K, M)) / np.sqrt(3 * K) / s, "e4m3")
    return {
        "tab": pack_table(n((K, T)) * s),
        "w0_words": p_w0[0],
        "w0_scales": p_w0[1],
        "w1_words": p_w1[0],
        "w1_scales": p_w1[1],
        "w2": (n((K, M)) / np.sqrt(3 * K) / s).astype(np.float32),
        "b": (0.3 * n(512)).astype(np.float32),
        "offs": striped(np.concatenate([np.random.permutation(T)[:S] for _ in range(3)])),
    }


def reference(tab, w0_words, w0_scales, w1_words, w1_scales, w2, b, offs):
    v = unpack_table(tab)
    idx = unstriped(offs).reshape(3, S)
    w0_ = unpack_weight(w0_words, w0_scales, "e2m1")
    w1_ = unpack_weight(w1_words, w1_scales, "e4m3")
    w2_ = mxq(f64(w2), 0, "e4m3")
    y = v[:, idx[0]].T @ w0_ + v[:, idx[1]].T @ w1_ + v[:, idx[2]].T @ w2_
    return gelu(y + f64(b)[None, :])

@@ -1,0 +1,222 @@
+from contextlib import ExitStack
+
+import concourse.mybir as mybir
+from concourse.masks import make_identity
+
+K, M, T, S = 1024, 512, 2048, 256
+FIELDS = 3
+FLOPS = 2 * FIELDS * K * M * S
+
+F32 = mybir.dt.float32
+BF16 = mybir.dt.bfloat16
+I32 = mybir.dt.int32
+U32 = mybir.dt.uint32
+U16 = mybir.dt.uint16
+U8 = mybir.dt.uint8
+FP8X4 = mybir.dt.float8_e4m3fn_x4
+FP4X4 = mybir.dt.float4_e2m1fn_x4
+
+P = 128
+PACK = 4
+K_PASS = P * PACK
+PASSES = K // K_PASS
+HALF = M // 2
+HALVES = 2
+TOKEN_TILES = S // P
+QUAD = 32
+ROWS = 4
+
+
+def tile_list_tabfield_tm_gelu_kernel(
+    tc, tab, w0_words, w0_scales, w1_words, w1_scales, w2, b, offs, out
+):
+    nc = tc.nc
+    with ExitStack() as ctx:
+        keep = ctx.enter_context(tc.tile_pool(name="keep", bufs=1))
+        psum = ctx.enter_context(tc.psum_pool(name="psum", bufs=1))
+
+        offsets = keep.tile([P, FIELDS * S // 16], U16, name="offsets")
+        nc.sync.dma_start(offsets[:], offs)
+
+        tab_scales = keep.tile([P, T // 4], I32, name="tab_scales", align_bytes=64)
+        w_scales = keep.tile([P, PASSES, M // 4], I32, name="w_scales", align_bytes=64)
+        nc.vector.memset(tab_scales[:, 0 : T // 8], 0)
+        nc.gpsimd.memset(tab_scales[:, T // 8 : T // 4], 0)
+        nc.vector.memset(w_scales[:], 0)
+
+        b_cols = keep.tile([P, PACK], F32, name="b_cols")
+        shifted_scales = keep.tile([P, S // 4], I32, name="shifted_scales", align_bytes=64)
+        nc.vector.memset(shifted_scales[:], 0)
+
+        tab_words = [keep.tile([P, T], I32, name=f"tab_words{a}", align_bytes=64) for a in range(PASSES)]
+        w2_raw = [
+            [keep.tile([P, PACK, HALF], F32, name=f"w2_raw{h}{a}", align_bytes=64) for a in range(PASSES)]
+            for h in range(HALVES)
+        ]
+        w0_codes = keep.tile([P, PASSES, 2 * M // 4], I32, name="w0_codes", align_bytes=64)
+        w1_codes = [keep.tile([P, PASSES, HALF], I32, name=f"w1_codes{h}", align_bytes=64) for h in range(HALVES)]
+
+        def load_table_words(a):
+            nc.sync.dma_start(
+                tab_words[a][:], tab[a, 0 : K_PASS * T].rearrange("(p w) -> p w", p=P).bitcast(I32)
+            )
+
+        def load_scale_rows(plane, first_row, rows):
+            for r in range(ROWS):
+                nc.sync.dma_start(plane[first_row + r : P : QUAD, :, :], rows[r : 16 : ROWS, :, :].bitcast(I32))
+
+        def load_w2(h, a):
+            rows = w2[a * K_PASS : (a + 1) * K_PASS, h * HALF : (h + 1) * HALF]
+            nc.sync.dma_start(w2_raw[h][a][:], rows.rearrange("(p j) n -> p j n", j=PACK))
+
+        def load_w1(h):
+            words = w1_words.rearrange("a p n i -> p a (n i)")[:, :, PACK * h * HALF : PACK * (h + 1) * HALF]
+            nc.sync.dma_start(w1_codes[h][:], words.bitcast(I32))
+
+        load_table_words(0)
+        b_rows = b.rearrange("(p c) -> p c", c=PACK)
+        nc.sync.dma_start(b_cols[:], b_rows)
+        tab_scale_rows = tab[:, K_PASS * T :].rearrange("a (q t) -> a q t", t=T)
+        for quad in range(P // QUAD):
+            nc.sync.dma_start(
+                tab_scales[QUAD * quad : QUAD * quad + PASSES * ROWS, :],
+                tab_scale_rows[:, ROWS * quad : ROWS * (quad + 1), :].bitcast(I32),
+            )
+        load_w2(0, 0)
+        load_table_words(1)
+        load_w2(0, 1)
+        load_scale_rows(w_scales, 0, w0_scales.rearrange("a q n -> q a n"))
+        nc.sync.dma_start(w0_codes[:], w0_words.rearrange("a p c -> p a c").bitcast(I32))
+        load_w2(1, 0)
+        load_w2(1, 1)
+        load_scale_rows(w_scales, ROWS, w1_scales.rearrange("a q n -> q a n"))
+        load_w1(0)
+        load_w1(1)
+
+        identity = keep.tile([P, P], F32, name="identity")
+        make_identity(nc, identity[:])
+        bias_bank = psum.tile([P, PACK, P], F32, name="bias_bank")
+        for c in range(PACK):
+            nc.tensor.transpose(bias_bank[:, c, :], b_cols[:, c : c + 1].to_broadcast([P, P]), identity[:])
+        bias = keep.tile([P, P, PACK], F32, name="bias")
+        nc.scalar.copy(bias[:], bias_bank[:].rearrange("j c p -> j p c"))
+        bias_row = bias[:].rearrange("j p c -> j (p c)")
+
+        picked_words = [keep.tile([P, FIELDS * S], U32, name=f"picked_words{a}", align_bytes=64) for a in range(PASSES)]
+        picked_scales = keep.tile([P, FIELDS * S], U8, name="picked_scales", align_bytes=64)
+
+        def gather(dst, window, fields):
+            for f in fields:
+                nc.vector.tensor_copy(
+                    dst[:, f * S : (f + 1) * S], window.indirect(offsets[:, f * S // 16 : (f + 1) * S // 16])
+                )
+
+        w2_bf16 = [
+            [keep.tile([P, HALF, PACK], BF16, name=f"w2_bf16{h}{a}", align_bytes=64) for a in range(PASSES)]
+            for h in range(HALVES)
+        ]
+        w2_codes = [
+            [keep.tile([P, HALF], U32, name=f"w2_codes{h}{a}", align_bytes=64) for a in range(PASSES)]
+            for h in range(HALVES)
+        ]
+        w2_scales = [
+            [keep.tile([P, HALF], U8, name=f"w2_scales{h}{a}", align_bytes=64) for a in range(PASSES)]
+            for h in range(HALVES)
+        ]
+
+        def interleave(copy, h, a, cols):
+            copy(
+                w2_bf16[h][a][:, cols, :].rearrange("p (c i) j -> p c j i", i=4),
+                w2_raw[h][a][:, :, cols].rearrange("p j (c i) -> p c j i", i=4),
+            )
+
+        def quantize(h, a):
+            nc.vector.quantize_mx(
+                out=w2_codes[h][a][:].bitcast(FP8X4),
+                scales=w2_scales[h][a][:],
+                in_=w2_bf16[h][a][:].rearrange("p n j -> p (n j)"),
+            )
+
+        tab_scale_bytes = tab_scales[:].bitcast(U8)
+        gather(picked_scales, tab_scale_bytes, (0,))
+        moved_rows = P - QUAD + ROWS
+        nc.gpsimd.dma_start(
+            shifted_scales[0:moved_rows, :], picked_scales[ROWS : ROWS + moved_rows, 0:S].bitcast(I32)
+        )
+        gather(picked_words[0], tab_words[0][:].bitcast(U32), (2, 0, 1))
+        gather(picked_scales, tab_scale_bytes, (2, 1))
+        interleave(nc.scalar.copy, 0, 0, slice(0, HALF))
+        quantize(0, 0)
+        interleave(nc.scalar.copy, 0, 1, slice(0, HALF))
+        gather(picked_words[1], tab_words[1][:].bitcast(U32), (2, 0, 1))
+        quantize(0, 1)
+        for a in range(PASSES):
+            interleave(nc.vector.tensor_copy, 1, a, slice(0, P))
+            interleave(nc.scalar.copy, 1, a, slice(P, HALF))
+            quantize(1, a)
+
+        w_scale_bytes = w_scales[:].bitcast(U8)
+        w0_bytes = w0_codes[:].bitcast(U8)
+        acc = [
+            [psum.tile([P, HALF], F32, name=f"acc{h}{tt}") for tt in range(TOKEN_TILES)] for h in range(HALVES)
+        ]
+
+        def table_pass(h, tt, f, a, cols, rhs, rhs_scale, start, stop):
+            tokens = slice(f * S + tt * P, f * S + (tt + 1) * P)
+            if (f, a) == (0, 1):
+                table_scale = shifted_scales[:].bitcast(U8)[:, tokens]
+            else:
+                table_scale = picked_scales[ROWS * a : P, tokens]
+            nc.tensor.matmul_mx(
+                out=acc[h][tt][:, cols],
+                lhsT=picked_words[a][:, tokens].bitcast(FP8X4),
+                lhsT_scale=table_scale,
+                rhs=rhs,
+                rhs_scale=rhs_scale,
+                start=start,
+                stop=stop,
+            )
+
+        def w2_passes(h, a, start):
+            for tt in range(TOKEN_TILES):
+                table_pass(
+                    h, tt, 2, a, slice(0, HALF), w2_codes[h][a][:].bitcast(FP8X4), w2_scales[h][a][:], start, False
+                )
+
+        def w0_passes(h, a, opens):
+            for tt in range(TOKEN_TILES):
+                for c0 in range(0, HALF, P):
+                    n0 = h * HALF + c0
+                    table_pass(
+                        h, tt, 0, a, slice(c0, c0 + P),
+                        w0_bytes[:, a, 2 * n0 : 2 * (n0 + P)].bitcast(FP4X4),
+                        w_scale_bytes[:, a, n0 : n0 + P], opens and c0 == 0, False,
+                    )
+
+        w2_passes(0, 0, True)
+        w0_passes(0, 0, False)
+        w0_passes(1, 0, True)
+        w2_passes(0, 1, False)
+        w2_passes(1, 0, False)
+        w0_passes(0, 1, False)
+        w0_passes(1, 1, False)
+        w2_passes(1, 1, False)
+
+        summed = [keep.tile([P, TOKEN_TILES, HALF], F32, name=f"summed{h}") for h in range(HALVES)]
+        result = [keep.tile([P, TOKEN_TILES, HALF], F32, name=f"result{h}") for h in range(HALVES)]
+        out_view = out.rearrange("(tt p) n -> p tt n", p=P)
+        for h in range(HALVES):
+            cols = slice(h * HALF, (h + 1) * HALF)
+            for tt in range(TOKEN_TILES):
+                for a in range(PASSES):
+                    table_pass(
+                        h, tt, 1, a, slice(0, HALF), w1_codes[h][:, a, :].bitcast(FP8X4),
+                        w_scale_bytes[ROWS:P, a, cols], False, a == PASSES - 1,
+                    )
+            for tt in range(TOKEN_TILES):
+                nc.vector.tensor_tensor(summed[h][:, tt, :], acc[h][tt][:], bias_row[:, cols], mybir.AluOpType.add)
+                nc.scalar.activation(result[h][:, tt, :], summed[h][:, tt, :], mybir.ActivationFunctionType.Gelu_apprx_tanh)
+                if h == HALVES - 1:
+                    nc.sync.dma_start(out_view[:, tt, cols], result[h][:, tt, :])
+            if h < HALVES - 1:
+                nc.sync.dma_start(out_view[:, :, cols], result[h][:])

@@ -25,6 +25,8 @@ HALVES = 2
 TOKEN_TILES = S // P
 QUAD = 32
 ROWS = 4
+KIB = 1024
+VECTOR_COLS = 168
 
 
 def tile_list_tabfield_tm_gelu_kernel(
@@ -33,65 +35,63 @@ def tile_list_tabfield_tm_gelu_kernel(
     nc = tc.nc
     with ExitStack() as ctx:
         keep = ctx.enter_context(tc.tile_pool(name="keep", bufs=1))
+        reuse = ctx.enter_context(tc.tile_pool(name="reuse", bufs=1))
         psum = ctx.enter_context(tc.psum_pool(name="psum", bufs=1))
 
         offsets = keep.tile([P, FIELDS * S // 16], U16, name="offsets")
         nc.sync.dma_start(offsets[:], offs)
 
-        tab_scales = keep.tile([P, T // 4], I32, name="tab_scales", align_bytes=64)
+        tab_scales = reuse.tile([P, T // 4], I32, name="tab_scales", align_bytes=64, offset=7 * KIB)
         w_scales = keep.tile([P, PASSES, M // 4], I32, name="w_scales", align_bytes=64)
+        shifted_scales = keep.tile([P, S // 4], I32, name="shifted_scales", align_bytes=64)
         nc.vector.memset(tab_scales[:, 0 : T // 8], 0)
         nc.gpsimd.memset(tab_scales[:, T // 8 : T // 4], 0)
         nc.vector.memset(w_scales[:], 0)
-
-        b_cols = keep.tile([P, PACK], F32, name="b_cols")
-        shifted_scales = keep.tile([P, S // 4], I32, name="shifted_scales", align_bytes=64)
         nc.vector.memset(shifted_scales[:], 0)
 
-        tab_words = [keep.tile([P, T], I32, name=f"tab_words{a}", align_bytes=64) for a in range(PASSES)]
-        w2_raw = [
-            [keep.tile([P, PACK, HALF], F32, name=f"w2_raw{h}{a}", align_bytes=64) for a in range(PASSES)]
-            for h in range(HALVES)
+        b_cols = keep.tile([P, PACK], F32, name="b_cols")
+        tab_words = [
+            keep.tile([P, T], I32, name="tab_words0", align_bytes=64),
+            reuse.tile([P, T], I32, name="tab_words1", align_bytes=64, offset=12 * KIB),
         ]
         w0_codes = keep.tile([P, PASSES, 2 * M // 4], I32, name="w0_codes", align_bytes=64)
-        w1_codes = [keep.tile([P, PASSES, HALF], I32, name=f"w1_codes{h}", align_bytes=64) for h in range(HALVES)]
+        w2_raw = [
+            keep.tile([P, PASSES, PACK, HALF], F32, name="w2_raw0", align_bytes=64),
+            reuse.tile([P, PASSES, PACK, HALF], F32, name="w2_raw1", align_bytes=64, offset=0),
+        ]
+        w1_codes = reuse.tile([P, PASSES, M], I32, name="w1_codes", align_bytes=64, offset=8 * KIB)
 
         def load_table_words(a):
             nc.sync.dma_start(
                 tab_words[a][:], tab[a, 0 : K_PASS * T].rearrange("(p w) -> p w", p=P).bitcast(I32)
             )
 
-        def load_scale_rows(plane, first_row, rows):
+        def load_scale_rows(first_row, rows):
             for r in range(ROWS):
-                nc.sync.dma_start(plane[first_row + r : P : QUAD, :, :], rows[r : 16 : ROWS, :, :].bitcast(I32))
+                nc.sync.dma_start(w_scales[first_row + r : P : QUAD, :, :], rows[r : 16 : ROWS, :, :].bitcast(I32))
 
         def load_w2(h, a):
             rows = w2[a * K_PASS : (a + 1) * K_PASS, h * HALF : (h + 1) * HALF]
-            nc.sync.dma_start(w2_raw[h][a][:], rows.rearrange("(p j) n -> p j n", j=PACK))
+            nc.sync.dma_start(w2_raw[h][:, a, :, :], rows.rearrange("(p j) n -> p j n", j=PACK))
 
-        def load_w1(h):
-            words = w1_words.rearrange("a p n i -> p a (n i)")[:, :, PACK * h * HALF : PACK * (h + 1) * HALF]
-            nc.sync.dma_start(w1_codes[h][:], words.bitcast(I32))
+        def load_w1(a, cols):
+            words = w1_words[a].rearrange("p n i -> p (n i)").bitcast(I32)
+            nc.sync.dma_start(w1_codes[:, a, cols], words[:, cols])
 
-        load_table_words(0)
-        b_rows = b.rearrange("(p c) -> p c", c=PACK)
-        nc.sync.dma_start(b_cols[:], b_rows)
+        nc.sync.dma_start(b_cols[:], b.rearrange("(p c) -> p c", c=PACK))
+        nc.sync.dma_start(w0_codes[:], w0_words.rearrange("a p c -> p a c").bitcast(I32))
         tab_scale_rows = tab[:, K_PASS * T :].rearrange("a (q t) -> a q t", t=T)
         for quad in range(P // QUAD):
             nc.sync.dma_start(
                 tab_scales[QUAD * quad : QUAD * quad + PASSES * ROWS, :],
                 tab_scale_rows[:, ROWS * quad : ROWS * (quad + 1), :].bitcast(I32),
             )
+        load_table_words(0)
         load_w2(0, 0)
+        load_scale_rows(0, w0_scales.rearrange("a q n -> q a n"))
         load_table_words(1)
+        load_scale_rows(ROWS, w1_scales.rearrange("a q n -> q a n"))
         load_w2(0, 1)
-        load_scale_rows(w_scales, 0, w0_scales.rearrange("a q n -> q a n"))
-        nc.sync.dma_start(w0_codes[:], w0_words.rearrange("a p c -> p a c").bitcast(I32))
-        load_w2(1, 0)
-        load_w2(1, 1)
-        load_scale_rows(w_scales, ROWS, w1_scales.rearrange("a q n -> q a n"))
-        load_w1(0)
-        load_w1(1)
 
         identity = keep.tile([P, P], F32, name="identity")
         make_identity(nc, identity[:])
@@ -102,8 +102,14 @@ def tile_list_tabfield_tm_gelu_kernel(
         nc.scalar.copy(bias[:], bias_bank[:].rearrange("j c p -> j p c"))
         bias_row = bias[:].rearrange("j p c -> j (p c)")
 
-        picked_words = [keep.tile([P, FIELDS * S], U32, name=f"picked_words{a}", align_bytes=64) for a in range(PASSES)]
         picked_scales = keep.tile([P, FIELDS * S], U8, name="picked_scales", align_bytes=64)
+        picked_words = [keep.tile([P, FIELDS * S], U32, name="picked_words0", align_bytes=64)]
+        w2_bf16 = {(0, 0): reuse.tile([P, HALF, PACK], BF16, name="w2_bf16_00", align_bytes=64, offset=20 * KIB)}
+        w2_codes = keep.tile([P, HALVES, PASSES, HALF], U32, name="w2_codes", align_bytes=64)
+        w2_scales = {
+            (h, a): keep.tile([P, HALF], U8, name=f"w2_scales_{h}{a}", align_bytes=64)
+            for h, a in ((0, 0), (1, 0), (1, 1))
+        }
 
         def gather(dst, window, fields):
             for f in fields:
@@ -111,49 +117,47 @@ def tile_list_tabfield_tm_gelu_kernel(
                     dst[:, f * S : (f + 1) * S], window.indirect(offsets[:, f * S // 16 : (f + 1) * S // 16])
                 )
 
-        w2_bf16 = [
-            [keep.tile([P, HALF, PACK], BF16, name=f"w2_bf16{h}{a}", align_bytes=64) for a in range(PASSES)]
-            for h in range(HALVES)
-        ]
-        w2_codes = [
-            [keep.tile([P, HALF], U32, name=f"w2_codes{h}{a}", align_bytes=64) for a in range(PASSES)]
-            for h in range(HALVES)
-        ]
-        w2_scales = [
-            [keep.tile([P, HALF], U8, name=f"w2_scales{h}{a}", align_bytes=64) for a in range(PASSES)]
-            for h in range(HALVES)
-        ]
-
         def interleave(copy, h, a, cols):
             copy(
-                w2_bf16[h][a][:, cols, :].rearrange("p (c i) j -> p c j i", i=4),
-                w2_raw[h][a][:, :, cols].rearrange("p j (c i) -> p c j i", i=4),
+                w2_bf16[h, a][:, cols, :].rearrange("p (c i) j -> p c j i", i=4),
+                w2_raw[h][:, a, :, cols].rearrange("p j (c i) -> p c j i", i=4),
             )
 
         def quantize(h, a):
             nc.vector.quantize_mx(
-                out=w2_codes[h][a][:].bitcast(FP8X4),
-                scales=w2_scales[h][a][:],
-                in_=w2_bf16[h][a][:].rearrange("p n j -> p (n j)"),
+                out=w2_codes[:, h, a, :].bitcast(FP8X4),
+                scales=w2_scales[h, a][:],
+                in_=w2_bf16[h, a][:].rearrange("p n j -> p (n j)"),
             )
 
-        tab_scale_bytes = tab_scales[:].bitcast(U8)
-        gather(picked_scales, tab_scale_bytes, (0,))
+        gather(picked_scales, tab_scales[:].bitcast(U8), (2, 1, 0))
+        gather(picked_words[0], tab_words[0][:].bitcast(U32), (2, 0, 1))
         moved_rows = P - QUAD + ROWS
-        nc.gpsimd.dma_start(
+        nc.sync.dma_start(
             shifted_scales[0:moved_rows, :], picked_scales[ROWS : ROWS + moved_rows, 0:S].bitcast(I32)
         )
-        gather(picked_words[0], tab_words[0][:].bitcast(U32), (2, 0, 1))
-        gather(picked_scales, tab_scale_bytes, (2, 1))
+        load_w2(1, 0)
+        load_w1(0, slice(0, M))
+        load_w2(1, 1)
+        load_w1(1, slice(0, HALF))
+        load_w1(1, slice(HALF, M))
         interleave(nc.scalar.copy, 0, 0, slice(0, HALF))
         quantize(0, 0)
-        interleave(nc.scalar.copy, 0, 1, slice(0, HALF))
-        gather(picked_words[1], tab_words[1][:].bitcast(U32), (2, 0, 1))
-        quantize(0, 1)
+        picked_words.append(reuse.tile([P, FIELDS * S], U32, name="picked_words1", align_bytes=64, offset=20 * KIB))
+        gather(picked_words[1], tab_words[1][:].bitcast(U32), (0, 2, 1))
+        w2_bf16[0, 1] = keep.tile([P, HALF, PACK], BF16, name="w2_bf16_01", align_bytes=64)
+        w2_scales[0, 1] = reuse.tile([P, HALF], U8, name="w2_scales_01", align_bytes=64, offset=12 * KIB)
         for a in range(PASSES):
-            interleave(nc.vector.tensor_copy, 1, a, slice(0, P))
-            interleave(nc.scalar.copy, 1, a, slice(P, HALF))
-            quantize(1, a)
+            w2_bf16[1, a] = reuse.tile(
+                [P, HALF, PACK], BF16, name=f"w2_bf16_1{a}", align_bytes=64, offset=(14 + 2 * a) * KIB
+            )
+        interleave(nc.scalar.copy, 0, 1, slice(0, HALF))
+        interleave(nc.vector.tensor_copy, 1, 0, slice(0, HALF))
+        quantize(0, 1)
+        quantize(1, 0)
+        interleave(nc.vector.tensor_copy, 1, 1, slice(0, VECTOR_COLS))
+        interleave(nc.scalar.copy, 1, 1, slice(VECTOR_COLS, HALF))
+        quantize(1, 1)
 
         w_scale_bytes = w_scales[:].bitcast(U8)
         w0_bytes = w0_codes[:].bitcast(U8)
@@ -177,10 +181,10 @@ def tile_list_tabfield_tm_gelu_kernel(
                 stop=stop,
             )
 
-        def w2_passes(h, a, start):
+        def w2_passes(h, a, start, stop=False):
             for tt in range(TOKEN_TILES):
                 table_pass(
-                    h, tt, 2, a, slice(0, HALF), w2_codes[h][a][:].bitcast(FP8X4), w2_scales[h][a][:], start, False
+                    h, tt, 2, a, slice(0, HALF), w2_codes[:, h, a, :].bitcast(FP8X4), w2_scales[h, a][:], start, stop
                 )
 
         def w0_passes(h, a, opens):
@@ -193,26 +197,32 @@ def tile_list_tabfield_tm_gelu_kernel(
                         w_scale_bytes[:, a, n0 : n0 + P], opens and c0 == 0, False,
                     )
 
+        def w1_pass(h, tt, a, stop):
+            cols = slice(h * HALF, (h + 1) * HALF)
+            table_pass(
+                h, tt, 1, a, slice(0, HALF), w1_codes[:, a, cols].bitcast(FP8X4), w_scale_bytes[ROWS:P, a, cols], False, stop
+            )
+
         w2_passes(0, 0, True)
         w0_passes(0, 0, False)
         w0_passes(1, 0, True)
-        w2_passes(0, 1, False)
-        w2_passes(1, 0, False)
         w0_passes(0, 1, False)
         w0_passes(1, 1, False)
-        w2_passes(1, 1, False)
+        w2_passes(0, 1, False)
+        w2_passes(1, 0, False)
+        for h in range(HALVES):
+            for tt in range(TOKEN_TILES):
+                w1_pass(h, tt, 0, False)
+        for h in range(HALVES):
+            for tt in range(TOKEN_TILES):
+                w1_pass(h, tt, 1, h == 0)
+        w2_passes(1, 1, False, True)
 
         summed = [keep.tile([P, TOKEN_TILES, HALF], F32, name=f"summed{h}") for h in range(HALVES)]
         result = [keep.tile([P, TOKEN_TILES, HALF], F32, name=f"result{h}") for h in range(HALVES)]
         out_view = out.rearrange("(tt p) n -> p tt n", p=P)
         for h in range(HALVES):
             cols = slice(h * HALF, (h + 1) * HALF)
-            for tt in range(TOKEN_TILES):
-                for a in range(PASSES):
-                    table_pass(
-                        h, tt, 1, a, slice(0, HALF), w1_codes[h][:, a, :].bitcast(FP8X4),
-                        w_scale_bytes[ROWS:P, a, cols], False, a == PASSES - 1,
-                    )
             for tt in range(TOKEN_TILES):
                 nc.vector.tensor_tensor(summed[h][:, tt, :], acc[h][tt][:], bias_row[:, cols], mybir.AluOpType.add)
                 nc.scalar.activation(result[h][:, tt, :], summed[h][:, tt, :], mybir.ActivationFunctionType.Gelu_apprx_tanh)

@@ -42,11 +42,13 @@ def tile_list_tabfield_tm_gelu_kernel(
         nc.sync.dma_start(offsets[:], offs)
 
         tab_scales = reuse.tile([P, T // 4], I32, name="tab_scales", align_bytes=64, offset=7 * KIB)
-        w_scales = keep.tile([P, PASSES, M // 4], I32, name="w_scales", align_bytes=64)
+        w0_plane = keep.tile([P, PASSES, M // 4], I32, name="w0_plane", align_bytes=64)
+        w1_plane = keep.tile([P, PASSES, M // 4], I32, name="w1_plane", align_bytes=64)
         shifted_scales = keep.tile([P, S // 4], I32, name="shifted_scales", align_bytes=64)
         nc.vector.memset(tab_scales[:, 0 : T // 8], 0)
         nc.gpsimd.memset(tab_scales[:, T // 8 : T // 4], 0)
-        nc.vector.memset(w_scales[:], 0)
+        nc.vector.memset(w0_plane[:], 0)
+        nc.vector.memset(w1_plane[:], 0)
         nc.vector.memset(shifted_scales[:], 0)
 
         b_cols = keep.tile([P, PACK], F32, name="b_cols")
@@ -55,10 +57,11 @@ def tile_list_tabfield_tm_gelu_kernel(
             reuse.tile([P, T], I32, name="tab_words1", align_bytes=64, offset=12 * KIB),
         ]
         w0_codes = keep.tile([P, PASSES, 2 * M // 4], I32, name="w0_codes", align_bytes=64)
-        w2_raw = [
-            keep.tile([P, PASSES, PACK, HALF], F32, name="w2_raw0", align_bytes=64),
-            reuse.tile([P, PASSES, PACK, HALF], F32, name="w2_raw1", align_bytes=64, offset=0),
-        ]
+        w2_raw0 = keep.tile([P, PACK, M], F32, name="w2_raw0", align_bytes=64)
+        w2_raw1 = reuse.tile([P, HALVES, PACK, HALF], F32, name="w2_raw1", align_bytes=64, offset=0)
+        w2_raw = {(h, 0): w2_raw0[:, :, h * HALF : (h + 1) * HALF] for h in range(HALVES)}
+        for h in range(HALVES):
+            w2_raw[h, 1] = w2_raw1[:, h, :, :]
         w1_codes = reuse.tile([P, PASSES, M], I32, name="w1_codes", align_bytes=64, offset=8 * KIB)
 
         def load_table_words(a):
@@ -66,13 +69,13 @@ def tile_list_tabfield_tm_gelu_kernel(
                 tab_words[a][:], tab[a, 0 : K_PASS * T].rearrange("(p w) -> p w", p=P).bitcast(I32)
             )
 
-        def load_scale_rows(first_row, rows):
+        def load_scale_rows(plane, first_row, rows):
             for r in range(ROWS):
-                nc.sync.dma_start(w_scales[first_row + r : P : QUAD, :, :], rows[r : 16 : ROWS, :, :].bitcast(I32))
+                nc.sync.dma_start(plane[first_row + r : P : QUAD, :, :], rows[r : 16 : ROWS, :, :].bitcast(I32))
 
-        def load_w2(h, a):
-            rows = w2[a * K_PASS : (a + 1) * K_PASS, h * HALF : (h + 1) * HALF]
-            nc.sync.dma_start(w2_raw[h][:, a, :, :], rows.rearrange("(p j) n -> p j n", j=PACK))
+        def load_w2(dst, a, cols):
+            rows = w2[a * K_PASS : (a + 1) * K_PASS, cols]
+            nc.sync.dma_start(dst, rows.rearrange("(p j) n -> p j n", j=PACK))
 
         def load_w1(a, cols):
             words = w1_words[a].rearrange("p n i -> p (n i)").bitcast(I32)
@@ -87,11 +90,10 @@ def tile_list_tabfield_tm_gelu_kernel(
                 tab_scale_rows[:, ROWS * quad : ROWS * (quad + 1), :].bitcast(I32),
             )
         load_table_words(0)
-        load_w2(0, 0)
-        load_scale_rows(0, w0_scales.rearrange("a q n -> q a n"))
+        load_w2(w2_raw0[:], 0, slice(0, M))
+        load_scale_rows(w0_plane, 0, w0_scales.rearrange("a q n -> q a n"))
         load_table_words(1)
-        load_scale_rows(ROWS, w1_scales.rearrange("a q n -> q a n"))
-        load_w2(0, 1)
+        load_scale_rows(w1_plane, ROWS, w1_scales.rearrange("a q n -> q a n"))
 
         identity = keep.tile([P, P], F32, name="identity")
         make_identity(nc, identity[:])
@@ -104,7 +106,10 @@ def tile_list_tabfield_tm_gelu_kernel(
 
         picked_scales = keep.tile([P, FIELDS * S], U8, name="picked_scales", align_bytes=64)
         picked_words = [keep.tile([P, FIELDS * S], U32, name="picked_words0", align_bytes=64)]
-        w2_bf16 = {(0, 0): reuse.tile([P, HALF, PACK], BF16, name="w2_bf16_00", align_bytes=64, offset=20 * KIB)}
+        w2_bf16 = {
+            (h, 0): reuse.tile([P, HALF, PACK], BF16, name=f"w2_bf16_{h}0", align_bytes=64, offset=(20 + 2 * h) * KIB)
+            for h in range(HALVES)
+        }
         w2_codes = keep.tile([P, HALVES, PASSES, HALF], U32, name="w2_codes", align_bytes=64)
         w2_scales = {
             (h, a): keep.tile([P, HALF], U8, name=f"w2_scales_{h}{a}", align_bytes=64)
@@ -117,17 +122,17 @@ def tile_list_tabfield_tm_gelu_kernel(
                     dst[:, f * S : (f + 1) * S], window.indirect(offsets[:, f * S // 16 : (f + 1) * S // 16])
                 )
 
-        def interleave(copy, h, a, cols):
+        def interleave(copy, h, a, cols, dst=None):
             copy(
-                w2_bf16[h, a][:, cols, :].rearrange("p (c i) j -> p c j i", i=4),
-                w2_raw[h][:, a, :, cols].rearrange("p j (c i) -> p c j i", i=4),
+                (w2_bf16[h, a][:, cols, :] if dst is None else dst).rearrange("p (c i) j -> p c j i", i=4),
+                w2_raw[h, a][:, :, cols].rearrange("p j (c i) -> p c j i", i=4),
             )
 
-        def quantize(h, a):
+        def quantize(h, a, cols=slice(0, HALF), src=None):
             nc.vector.quantize_mx(
-                out=w2_codes[:, h, a, :].bitcast(FP8X4),
-                scales=w2_scales[h, a][:],
-                in_=w2_bf16[h, a][:].rearrange("p n j -> p (n j)"),
+                out=w2_codes[:, h, a, cols].bitcast(FP8X4),
+                scales=w2_scales[h, a][:, cols],
+                in_=(w2_bf16[h, a][:] if src is None else src).rearrange("p n j -> p (n j)"),
             )
 
         gather(picked_scales, tab_scales[:].bitcast(U8), (2, 1, 0))
@@ -136,30 +141,31 @@ def tile_list_tabfield_tm_gelu_kernel(
         nc.sync.dma_start(
             shifted_scales[0:moved_rows, :], picked_scales[ROWS : ROWS + moved_rows, 0:S].bitcast(I32)
         )
-        load_w2(1, 0)
+        load_w2(w2_raw[0, 1], 1, slice(0, HALF))
         load_w1(0, slice(0, M))
-        load_w2(1, 1)
+        load_w2(w2_raw[1, 1], 1, slice(HALF, M))
         load_w1(1, slice(0, HALF))
         load_w1(1, slice(HALF, M))
         interleave(nc.scalar.copy, 0, 0, slice(0, HALF))
+        interleave(nc.vector.tensor_copy, 1, 0, slice(0, HALF))
+        quantize(1, 0)
         quantize(0, 0)
         picked_words.append(reuse.tile([P, FIELDS * S], U32, name="picked_words1", align_bytes=64, offset=20 * KIB))
         gather(picked_words[1], tab_words[1][:].bitcast(U32), (0, 2, 1))
-        w2_bf16[0, 1] = keep.tile([P, HALF, PACK], BF16, name="w2_bf16_01", align_bytes=64)
+        early = keep.tile([P, P, PACK], BF16, name="w2_bf16_01s", align_bytes=64)
+        late = reuse.tile([P, P, PACK], BF16, name="w2_bf16_01v", align_bytes=64, offset=16 * KIB)
         w2_scales[0, 1] = reuse.tile([P, HALF], U8, name="w2_scales_01", align_bytes=64, offset=12 * KIB)
-        for a in range(PASSES):
-            w2_bf16[1, a] = reuse.tile(
-                [P, HALF, PACK], BF16, name=f"w2_bf16_1{a}", align_bytes=64, offset=(14 + 2 * a) * KIB
-            )
-        interleave(nc.scalar.copy, 0, 1, slice(0, HALF))
-        interleave(nc.vector.tensor_copy, 1, 0, slice(0, HALF))
-        quantize(0, 1)
-        quantize(1, 0)
+        w2_bf16[1, 1] = reuse.tile([P, HALF, PACK], BF16, name="w2_bf16_11", align_bytes=64, offset=14 * KIB)
+        interleave(nc.scalar.copy, 0, 1, slice(0, P), early[:])
+        interleave(nc.vector.tensor_copy, 0, 1, slice(P, HALF), late[:])
+        quantize(0, 1, slice(0, P), early[:])
+        quantize(0, 1, slice(P, HALF), late[:])
         interleave(nc.vector.tensor_copy, 1, 1, slice(0, VECTOR_COLS))
         interleave(nc.scalar.copy, 1, 1, slice(VECTOR_COLS, HALF))
         quantize(1, 1)
 
-        w_scale_bytes = w_scales[:].bitcast(U8)
+        w0_scale_bytes = w0_plane[:].bitcast(U8)
+        w1_scale_bytes = w1_plane[:].bitcast(U8)
         w0_bytes = w0_codes[:].bitcast(U8)
         acc = [
             [psum.tile([P, HALF], F32, name=f"acc{h}{tt}") for tt in range(TOKEN_TILES)] for h in range(HALVES)
@@ -194,25 +200,25 @@ def tile_list_tabfield_tm_gelu_kernel(
                     table_pass(
                         h, tt, 0, a, slice(c0, c0 + P),
                         w0_bytes[:, a, 2 * n0 : 2 * (n0 + P)].bitcast(FP4X4),
-                        w_scale_bytes[:, a, n0 : n0 + P], opens and c0 == 0, False,
+                        w0_scale_bytes[:, a, n0 : n0 + P], opens and c0 == 0, False,
                     )
 
         def w1_pass(h, tt, a, stop):
             cols = slice(h * HALF, (h + 1) * HALF)
             table_pass(
-                h, tt, 1, a, slice(0, HALF), w1_codes[:, a, cols].bitcast(FP8X4), w_scale_bytes[ROWS:P, a, cols], False, stop
+                h, tt, 1, a, slice(0, HALF), w1_codes[:, a, cols].bitcast(FP8X4), w1_scale_bytes[ROWS:P, a, cols], False, stop
             )
 
-        w2_passes(0, 0, True)
-        w0_passes(0, 0, False)
-        w0_passes(1, 0, True)
-        w0_passes(0, 1, False)
-        w0_passes(1, 1, False)
-        w2_passes(0, 1, False)
+        for h in range(HALVES):
+            w0_passes(h, 0, True)
         w2_passes(1, 0, False)
+        w2_passes(0, 0, False)
+        for h in range(HALVES):
+            w0_passes(h, 1, False)
         for h in range(HALVES):
             for tt in range(TOKEN_TILES):
                 w1_pass(h, tt, 0, False)
+        w2_passes(0, 1, False)
         for h in range(HALVES):
             for tt in range(TOKEN_TILES):
                 w1_pass(h, tt, 1, h == 0)

@@ -90,10 +90,10 @@ def tile_list_tabfield_tm_gelu_kernel(
                 tab_scale_rows[:, ROWS * quad : ROWS * (quad + 1), :].bitcast(I32),
             )
         load_table_words(0)
-        load_w2(w2_raw0[:], 0, slice(0, M))
         load_scale_rows(w0_plane, 0, w0_scales.rearrange("a q n -> q a n"))
-        load_table_words(1)
+        load_w2(w2_raw0[:], 0, slice(0, M))
         load_scale_rows(w1_plane, ROWS, w1_scales.rearrange("a q n -> q a n"))
+        load_table_words(1)
 
         identity = keep.tile([P, P], F32, name="identity")
         make_identity(nc, identity[:])
@@ -142,8 +142,8 @@ def tile_list_tabfield_tm_gelu_kernel(
             shifted_scales[0:moved_rows, :], picked_scales[ROWS : ROWS + moved_rows, 0:S].bitcast(I32)
         )
         load_w2(w2_raw[0, 1], 1, slice(0, HALF))
-        load_w1(0, slice(0, M))
         load_w2(w2_raw[1, 1], 1, slice(HALF, M))
+        load_w1(0, slice(0, M))
         load_w1(1, slice(0, HALF))
         load_w1(1, slice(HALF, M))
         interleave(nc.scalar.copy, 0, 0, slice(0, HALF))
@@ -211,18 +211,19 @@ def tile_list_tabfield_tm_gelu_kernel(
 
         for h in range(HALVES):
             w0_passes(h, 0, True)
-        w2_passes(1, 0, False)
-        w2_passes(0, 0, False)
         for h in range(HALVES):
             w0_passes(h, 1, False)
         for h in range(HALVES):
-            for tt in range(TOKEN_TILES):
-                w1_pass(h, tt, 0, False)
+            w2_passes(h, 0, False)
         w2_passes(0, 1, False)
         for h in range(HALVES):
             for tt in range(TOKEN_TILES):
-                w1_pass(h, tt, 1, h == 0)
-        w2_passes(1, 1, False, True)
+                w1_pass(h, tt, 0, False)
+        for tt in range(TOKEN_TILES):
+            w1_pass(0, tt, 1, True)
+        w2_passes(1, 1, False)
+        for tt in range(TOKEN_TILES):
+            w1_pass(1, tt, 1, True)
 
         summed = [keep.tile([P, TOKEN_TILES, HALF], F32, name=f"summed{h}") for h in range(HALVES)]
         result = [keep.tile([P, TOKEN_TILES, HALF], F32, name=f"result{h}") for h in range(HALVES)]

@@ -26,7 +26,8 @@ TOKEN_TILES = S // P
 QUAD = 32
 ROWS = 4
 KIB = 1024
-VECTOR_COLS = 168
+VECTOR_COLS_FIRST = 64
+VECTOR_COLS = 116
 
 
 def tile_list_tabfield_tm_gelu_kernel(
@@ -38,62 +39,55 @@ def tile_list_tabfield_tm_gelu_kernel(
         reuse = ctx.enter_context(tc.tile_pool(name="reuse", bufs=1))
         psum = ctx.enter_context(tc.psum_pool(name="psum", bufs=1))
 
-        offsets = keep.tile([P, FIELDS * S // 16], U16, name="offsets")
-        nc.sync.dma_start(offsets[:], offs)
-
-        tab_scales = reuse.tile([P, T // 4], I32, name="tab_scales", align_bytes=64, offset=7 * KIB)
-        w0_plane = keep.tile([P, PASSES, M // 4], I32, name="w0_plane", align_bytes=64)
-        w1_plane = keep.tile([P, PASSES, M // 4], I32, name="w1_plane", align_bytes=64)
+        tab_scales = reuse.tile([P, T // 4], I32, name="tab_scales", align_bytes=64, offset=8 * KIB)
+        w_planes = keep.tile([P, 2, PASSES, M // 4], I32, name="w_planes", align_bytes=64)
         shifted_scales = keep.tile([P, S // 4], I32, name="shifted_scales", align_bytes=64)
         nc.vector.memset(tab_scales[:, 0 : T // 8], 0)
         nc.gpsimd.memset(tab_scales[:, T // 8 : T // 4], 0)
-        nc.vector.memset(w0_plane[:], 0)
-        nc.vector.memset(w1_plane[:], 0)
+        nc.vector.memset(w_planes[:], 0)
         nc.vector.memset(shifted_scales[:], 0)
 
+        offsets = keep.tile([P, FIELDS * S // 16], U16, name="offsets")
         b_cols = keep.tile([P, PACK], F32, name="b_cols")
         tab_words = [
-            keep.tile([P, T], I32, name="tab_words0", align_bytes=64),
-            reuse.tile([P, T], I32, name="tab_words1", align_bytes=64, offset=12 * KIB),
+            reuse.tile([P, T], I32, name="tab_words0", align_bytes=64, offset=16 * KIB),
+            reuse.tile([P, T], I32, name="tab_words1", align_bytes=64, offset=32 * KIB),
         ]
         w0_codes = keep.tile([P, PASSES, 2 * M // 4], I32, name="w0_codes", align_bytes=64)
         w2_raw0 = keep.tile([P, PACK, M], F32, name="w2_raw0", align_bytes=64)
-        w2_raw1 = reuse.tile([P, HALVES, PACK, HALF], F32, name="w2_raw1", align_bytes=64, offset=0)
         w2_raw = {(h, 0): w2_raw0[:, :, h * HALF : (h + 1) * HALF] for h in range(HALVES)}
-        for h in range(HALVES):
-            w2_raw[h, 1] = w2_raw1[:, h, :, :]
-        w1_codes = reuse.tile([P, PASSES, M], I32, name="w1_codes", align_bytes=64, offset=8 * KIB)
 
         def load_table_words(a):
             nc.sync.dma_start(
                 tab_words[a][:], tab[a, 0 : K_PASS * T].rearrange("(p w) -> p w", p=P).bitcast(I32)
             )
 
-        def load_scale_rows(plane, first_row, rows):
-            for r in range(ROWS):
-                nc.sync.dma_start(plane[first_row + r : P : QUAD, :, :], rows[r : 16 : ROWS, :, :].bitcast(I32))
+        def load_table_scales(queue):
+            tab_scale_rows = tab[:, K_PASS * T :].rearrange("a (q t) -> a q t", t=T)
+            for quad in range(P // QUAD):
+                queue.dma_start(
+                    tab_scales[QUAD * quad : QUAD * quad + PASSES * ROWS, :],
+                    tab_scale_rows[:, ROWS * quad : ROWS * (quad + 1), :].bitcast(I32),
+                )
 
         def load_w2(dst, a, cols):
             rows = w2[a * K_PASS : (a + 1) * K_PASS, cols]
             nc.sync.dma_start(dst, rows.rearrange("(p j) n -> p j n", j=PACK))
 
-        def load_w1(a, cols):
-            words = w1_words[a].rearrange("p n i -> p (n i)").bitcast(I32)
-            nc.sync.dma_start(w1_codes[:, a, cols], words[:, cols])
-
+        nc.sync.dma_start(offsets[:], offs)
         nc.sync.dma_start(b_cols[:], b.rearrange("(p c) -> p c", c=PACK))
         nc.sync.dma_start(w0_codes[:], w0_words.rearrange("a p c -> p a c").bitcast(I32))
-        tab_scale_rows = tab[:, K_PASS * T :].rearrange("a (q t) -> a q t", t=T)
-        for quad in range(P // QUAD):
-            nc.sync.dma_start(
-                tab_scales[QUAD * quad : QUAD * quad + PASSES * ROWS, :],
-                tab_scale_rows[:, ROWS * quad : ROWS * (quad + 1), :].bitcast(I32),
-            )
+        load_table_scales(nc.sync)
         load_table_words(0)
-        load_scale_rows(w0_plane, 0, w0_scales.rearrange("a q n -> q a n"))
+        for f, scales in enumerate((w0_scales, w1_scales)):
+            nc.sync.dma_start(w_planes[0:16, f, :, :], scales.rearrange("a q n -> q a n").bitcast(I32))
         load_w2(w2_raw0[:], 0, slice(0, M))
-        load_scale_rows(w1_plane, ROWS, w1_scales.rearrange("a q n -> q a n"))
         load_table_words(1)
+        for quad in range(1, P // QUAD):
+            nc.scalar.dma_start(
+                w_planes[QUAD * quad : QUAD * quad + ROWS, :, :, :].rearrange("p f a n -> p (f a n)"),
+                w_planes[ROWS * quad : ROWS * (quad + 1), :, :, :].rearrange("p f a n -> p (f a n)"),
+            )
 
         identity = keep.tile([P, P], F32, name="identity")
         make_identity(nc, identity[:])
@@ -104,17 +98,14 @@ def tile_list_tabfield_tm_gelu_kernel(
         nc.scalar.copy(bias[:], bias_bank[:].rearrange("j c p -> j p c"))
         bias_row = bias[:].rearrange("j p c -> j (p c)")
 
-        picked_scales = keep.tile([P, FIELDS * S], U8, name="picked_scales", align_bytes=64)
         picked_words = [keep.tile([P, FIELDS * S], U32, name="picked_words0", align_bytes=64)]
-        w2_bf16 = {
-            (h, 0): reuse.tile([P, HALF, PACK], BF16, name=f"w2_bf16_{h}0", align_bytes=64, offset=(20 + 2 * h) * KIB)
-            for h in range(HALVES)
-        }
         w2_codes = keep.tile([P, HALVES, PASSES, HALF], U32, name="w2_codes", align_bytes=64)
         w2_scales = {
             (h, a): keep.tile([P, HALF], U8, name=f"w2_scales_{h}{a}", align_bytes=64)
-            for h, a in ((0, 0), (1, 0), (1, 1))
+            for h in range(HALVES)
+            for a in range(PASSES)
         }
+        w2_bf16 = {}
 
         def gather(dst, window, fields):
             for f in fields:
@@ -135,37 +126,41 @@ def tile_list_tabfield_tm_gelu_kernel(
                 in_=(w2_bf16[h, a][:] if src is None else src).rearrange("p n j -> p (n j)"),
             )
 
-        gather(picked_scales, tab_scales[:].bitcast(U8), (2, 1, 0))
-        gather(picked_words[0], tab_words[0][:].bitcast(U32), (2, 0, 1))
+        picked_scales = keep.tile([P, FIELDS * S], U8, name="picked_scales", align_bytes=64)
+        gather(picked_scales, tab_scales[:].bitcast(U8), (0, 2, 1))
+        gather(picked_words[0], tab_words[0][:].bitcast(U32), (0, 2, 1))
         moved_rows = P - QUAD + ROWS
         nc.sync.dma_start(
             shifted_scales[0:moved_rows, :], picked_scales[ROWS : ROWS + moved_rows, 0:S].bitcast(I32)
         )
-        load_w2(w2_raw[0, 1], 1, slice(0, HALF))
-        load_w2(w2_raw[1, 1], 1, slice(HALF, M))
-        load_w1(0, slice(0, M))
-        load_w1(1, slice(0, HALF))
-        load_w1(1, slice(HALF, M))
+        for h in range(HALVES):
+            raw = reuse.tile([P, PACK, HALF], F32, name=f"w2_raw1_{h}", align_bytes=64, offset=(12 + 4 * h) * KIB + 64)
+            w2_raw[h, 1] = raw[:]
+            load_w2(raw[:], 1, slice(h * HALF, (h + 1) * HALF))
+        w1_codes = []
+        w1_rows = w1_words.rearrange("a p n i -> p a (n i)").bitcast(I32)
+        for h, start in enumerate((20 * KIB + 64, 23 * KIB)):
+            w1_codes.append(reuse.tile([P, PASSES, HALF], I32, name=f"w1_codes{h}", align_bytes=64, offset=start))
+            nc.sync.dma_start(w1_codes[h][:], w1_rows[:, :, h * HALF : (h + 1) * HALF])
+        w2_bf16[0, 0] = reuse.tile([P, HALF, PACK], BF16, name="w2_bf16_00", align_bytes=64, offset=2 * KIB)
+        w2_bf16[1, 0] = reuse.tile([P, HALF, PACK], BF16, name="w2_bf16_10", align_bytes=64, offset=0)
         interleave(nc.scalar.copy, 0, 0, slice(0, HALF))
         interleave(nc.vector.tensor_copy, 1, 0, slice(0, HALF))
         quantize(1, 0)
         quantize(0, 0)
-        picked_words.append(reuse.tile([P, FIELDS * S], U32, name="picked_words1", align_bytes=64, offset=20 * KIB))
+        picked_words.append(reuse.tile([P, FIELDS * S], U32, name="picked_words1", align_bytes=64, offset=1 * KIB))
         gather(picked_words[1], tab_words[1][:].bitcast(U32), (0, 2, 1))
-        early = keep.tile([P, P, PACK], BF16, name="w2_bf16_01s", align_bytes=64)
-        late = reuse.tile([P, P, PACK], BF16, name="w2_bf16_01v", align_bytes=64, offset=16 * KIB)
-        w2_scales[0, 1] = reuse.tile([P, HALF], U8, name="w2_scales_01", align_bytes=64, offset=12 * KIB)
-        w2_bf16[1, 1] = reuse.tile([P, HALF, PACK], BF16, name="w2_bf16_11", align_bytes=64, offset=14 * KIB)
-        interleave(nc.scalar.copy, 0, 1, slice(0, P), early[:])
-        interleave(nc.vector.tensor_copy, 0, 1, slice(P, HALF), late[:])
-        quantize(0, 1, slice(0, P), early[:])
-        quantize(0, 1, slice(P, HALF), late[:])
+        for h in range(HALVES):
+            w2_bf16[h, 1] = keep.tile([P, HALF, PACK], BF16, name=f"w2_bf16_{h}1", align_bytes=64)
+        interleave(nc.scalar.copy, 0, 1, slice(0, HALF - VECTOR_COLS_FIRST))
+        interleave(nc.vector.tensor_copy, 0, 1, slice(HALF - VECTOR_COLS_FIRST, HALF))
+        quantize(0, 1)
         interleave(nc.vector.tensor_copy, 1, 1, slice(0, VECTOR_COLS))
         interleave(nc.scalar.copy, 1, 1, slice(VECTOR_COLS, HALF))
         quantize(1, 1)
 
-        w0_scale_bytes = w0_plane[:].bitcast(U8)
-        w1_scale_bytes = w1_plane[:].bitcast(U8)
+        w0_scale_bytes = w_planes[:, 0, :, :].bitcast(U8)
+        w1_scale_bytes = w_planes[:, 1, :, :].bitcast(U8)
         w0_bytes = w0_codes[:].bitcast(U8)
         acc = [
             [psum.tile([P, HALF], F32, name=f"acc{h}{tt}") for tt in range(TOKEN_TILES)] for h in range(HALVES)
@@ -187,13 +182,13 @@ def tile_list_tabfield_tm_gelu_kernel(
                 stop=stop,
             )
 
-        def w2_passes(h, a, start, stop=False):
+        def w2_passes(h, a, start):
             for tt in range(TOKEN_TILES):
                 table_pass(
-                    h, tt, 2, a, slice(0, HALF), w2_codes[:, h, a, :].bitcast(FP8X4), w2_scales[h, a][:], start, stop
+                    h, tt, 2, a, slice(0, HALF), w2_codes[:, h, a, :].bitcast(FP8X4), w2_scales[h, a][:], start, False
                 )
 
-        def w0_passes(h, a, opens):
+        def w0_passes(h, a, opens=False):
             for tt in range(TOKEN_TILES):
                 for c0 in range(0, HALF, P):
                     n0 = h * HALF + c0
@@ -203,27 +198,24 @@ def tile_list_tabfield_tm_gelu_kernel(
                         w0_scale_bytes[:, a, n0 : n0 + P], opens and c0 == 0, False,
                     )
 
-        def w1_pass(h, tt, a, stop):
+        def w1_passes(h):
             cols = slice(h * HALF, (h + 1) * HALF)
-            table_pass(
-                h, tt, 1, a, slice(0, HALF), w1_codes[:, a, cols].bitcast(FP8X4), w1_scale_bytes[ROWS:P, a, cols], False, stop
-            )
-
-        for h in range(HALVES):
-            w0_passes(h, 0, True)
-        for h in range(HALVES):
-            w0_passes(h, 1, False)
-        for h in range(HALVES):
-            w2_passes(h, 0, False)
-        w2_passes(0, 1, False)
-        for h in range(HALVES):
             for tt in range(TOKEN_TILES):
-                w1_pass(h, tt, 0, False)
-        for tt in range(TOKEN_TILES):
-            w1_pass(0, tt, 1, True)
+                for a in range(PASSES):
+                    table_pass(
+                        h, tt, 1, a, slice(0, HALF), w1_codes[h][:, a, :].bitcast(FP8X4),
+                        w1_scale_bytes[:, a, cols], False, a == PASSES - 1,
+                    )
+
+        w2_passes(1, 0, True)
+        w2_passes(0, 0, True)
+        for a in range(PASSES):
+            for h in range(HALVES):
+                w0_passes(h, a)
+        w2_passes(0, 1, False)
+        w1_passes(0)
         w2_passes(1, 1, False)
-        for tt in range(TOKEN_TILES):
-            w1_pass(1, tt, 1, True)
+        w1_passes(1)
 
         summed = [keep.tile([P, TOKEN_TILES, HALF], F32, name=f"summed{h}") for h in range(HALVES)]
         result = [keep.tile([P, TOKEN_TILES, HALF], F32, name=f"result{h}") for h in range(HALVES)]

@@ -26,8 +26,9 @@ TOKEN_TILES = S // P
 QUAD = 32
 ROWS = 4
 KIB = 1024
-VECTOR_COLS_FIRST = 64
-VECTOR_COLS = 116
+LIVE = P - PASSES * 16
+PLANE = M + FIELDS * S
+VECTOR_COLS = (120, 144)
 
 
 def tile_list_tabfield_tm_gelu_kernel(
@@ -39,13 +40,18 @@ def tile_list_tabfield_tm_gelu_kernel(
         reuse = ctx.enter_context(tc.tile_pool(name="reuse", bufs=1))
         psum = ctx.enter_context(tc.psum_pool(name="psum", bufs=1))
 
-        tab_scales = reuse.tile([P, T // 4], I32, name="tab_scales", align_bytes=64, offset=8 * KIB)
-        w_planes = keep.tile([P, 2, PASSES, M // 4], I32, name="w_planes", align_bytes=64)
-        shifted_scales = keep.tile([P, S // 4], I32, name="shifted_scales", align_bytes=64)
-        nc.vector.memset(tab_scales[:, 0 : T // 8], 0)
-        nc.gpsimd.memset(tab_scales[:, T // 8 : T // 4], 0)
-        nc.vector.memset(w_planes[:], 0)
-        nc.vector.memset(shifted_scales[:], 0)
+        scale_window = keep.tile([P, T // 4], I32, name="scale_window", align_bytes=64)
+        staged = keep.tile([P, PLANE // 4], I32, name="staged", align_bytes=64)
+        planes = keep.tile([P, PASSES, PLANE // 4], I32, name="planes", align_bytes=64)
+        nc.vector.memset(scale_window[0:LIVE, :], 0)
+        w1_planes = keep.tile([P, PASSES, M // 4], I32, name="w1_planes", align_bytes=64)
+        nc.vector.memset(w1_planes[:], 0)
+        nc.vector.memset(planes[:], 0)
+        for quad in range(P // QUAD):
+            nc.gpsimd.dma_start(
+                w1_planes[QUAD * quad + ROWS : QUAD * quad + 2 * ROWS, :, :],
+                w1_scales[:, ROWS * quad : ROWS * (quad + 1), :].rearrange("a r n -> r a n").bitcast(I32),
+            )
 
         offsets = keep.tile([P, FIELDS * S // 16], U16, name="offsets")
         b_cols = keep.tile([P, PACK], F32, name="b_cols")
@@ -57,37 +63,66 @@ def tile_list_tabfield_tm_gelu_kernel(
         w2_raw0 = keep.tile([P, PACK, M], F32, name="w2_raw0", align_bytes=64)
         w2_raw = {(h, 0): w2_raw0[:, :, h * HALF : (h + 1) * HALF] for h in range(HALVES)}
 
-        def load_table_words(a):
-            nc.sync.dma_start(
-                tab_words[a][:], tab[a, 0 : K_PASS * T].rearrange("(p w) -> p w", p=P).bitcast(I32)
-            )
-
-        def load_table_scales(queue):
-            tab_scale_rows = tab[:, K_PASS * T :].rearrange("a (q t) -> a q t", t=T)
-            for quad in range(P // QUAD):
-                queue.dma_start(
-                    tab_scales[QUAD * quad : QUAD * quad + PASSES * ROWS, :],
-                    tab_scale_rows[:, ROWS * quad : ROWS * (quad + 1), :].bitcast(I32),
-                )
-
         def load_w2(dst, a, cols):
             rows = w2[a * K_PASS : (a + 1) * K_PASS, cols]
             nc.sync.dma_start(dst, rows.rearrange("(p j) n -> p j n", j=PACK))
 
         nc.sync.dma_start(offsets[:], offs)
+        nc.sync.dma_start(
+            scale_window[LIVE:P, :], tab[:, K_PASS * T :].rearrange("a (q t) -> q a t", t=T).bitcast(I32)
+        )
+        nc.sync.dma_start(staged[LIVE:P, 0 : M // 4], w0_scales.rearrange("a q n -> q a n").bitcast(I32))
         nc.sync.dma_start(b_cols[:], b.rearrange("(p c) -> p c", c=PACK))
-        nc.sync.dma_start(w0_codes[:], w0_words.rearrange("a p c -> p a c").bitcast(I32))
-        load_table_scales(nc.sync)
-        load_table_words(0)
-        for f, scales in enumerate((w0_scales, w1_scales)):
-            nc.sync.dma_start(w_planes[0:16, f, :, :], scales.rearrange("a q n -> q a n").bitcast(I32))
-        load_w2(w2_raw0[:], 0, slice(0, M))
-        load_table_words(1)
-        for quad in range(1, P // QUAD):
-            nc.scalar.dma_start(
-                w_planes[QUAD * quad : QUAD * quad + ROWS, :, :, :].rearrange("p f a n -> p (f a n)"),
-                w_planes[ROWS * quad : ROWS * (quad + 1), :, :, :].rearrange("p f a n -> p (f a n)"),
+        for a in range(PASSES):
+            nc.sync.dma_start(
+                tab_words[a][:], tab[a, 0 : K_PASS * T].rearrange("(p w) -> p w", p=P).bitcast(I32)
             )
+        nc.sync.dma_start(w0_codes[:], w0_words.rearrange("a p c -> p a c").bitcast(I32))
+        load_w2(w2_raw0[:], 0, slice(0, M))
+
+        picked_words = [keep.tile([P, FIELDS * S], U32, name=f"picked_words{a}", align_bytes=64) for a in range(PASSES)]
+        picked_scales = keep.tile([P, FIELDS * S], U8, name="picked_scales", align_bytes=64)
+        w2_codes = keep.tile([P, HALVES, PASSES, HALF], U32, name="w2_codes", align_bytes=64)
+        w2_scales = {
+            (h, a): keep.tile([P, HALF], U8, name=f"w2_scales_{h}{a}", align_bytes=64)
+            for h in range(HALVES)
+            for a in range(PASSES)
+        }
+        w2_bf16 = {
+            (h, a): keep.tile([P, HALF, PACK], BF16, name=f"w2_bf16_{h}{a}", align_bytes=64)
+            for h in range(HALVES)
+            for a in range(PASSES)
+        }
+
+        def gather(dst, window, first, last):
+            nc.vector.tensor_copy(
+                dst[:, first * S : last * S], window.indirect(offsets[:, first * S // 16 : last * S // 16])
+            )
+
+        def interleave(copy, h, a, cols):
+            copy(
+                w2_bf16[h, a][:, cols, :].rearrange("p (c i) j -> p c j i", i=4),
+                w2_raw[h, a][:, :, cols].rearrange("p j (c i) -> p c j i", i=4),
+            )
+
+        def quantize(h, a):
+            nc.vector.quantize_mx(
+                out=w2_codes[:, h, a, :].bitcast(FP8X4),
+                scales=w2_scales[h, a][:],
+                in_=w2_bf16[h, a][:].rearrange("p n j -> p (n j)"),
+            )
+
+        gather(picked_scales, scale_window[:].bitcast(U8), 0, FIELDS)
+        nc.vector.tensor_copy(staged[LIVE:P, M // 4 : PLANE // 4], picked_scales[LIVE:P, :].bitcast(I32))
+        for quad in (0, 2, 1, 3):
+            first = LIVE + PASSES * ROWS * quad
+            nc.scalar.dma_start(
+                planes[QUAD * quad : QUAD * quad + ROWS, :, :].rearrange("p a n -> p (a n)"),
+                staged[first : first + PASSES * ROWS, :],
+            )
+        gather(picked_words[0], tab_words[0][:].bitcast(U32), 0, FIELDS)
+        gather(picked_words[1], tab_words[1][:].bitcast(U32), 0, 1)
+        gather(picked_words[1], tab_words[1][:].bitcast(U32), 1, FIELDS)
 
         identity = keep.tile([P, P], F32, name="identity")
         make_identity(nc, identity[:])
@@ -98,41 +133,6 @@ def tile_list_tabfield_tm_gelu_kernel(
         nc.scalar.copy(bias[:], bias_bank[:].rearrange("j c p -> j p c"))
         bias_row = bias[:].rearrange("j p c -> j (p c)")
 
-        picked_words = [keep.tile([P, FIELDS * S], U32, name="picked_words0", align_bytes=64)]
-        w2_codes = keep.tile([P, HALVES, PASSES, HALF], U32, name="w2_codes", align_bytes=64)
-        w2_scales = {
-            (h, a): keep.tile([P, HALF], U8, name=f"w2_scales_{h}{a}", align_bytes=64)
-            for h in range(HALVES)
-            for a in range(PASSES)
-        }
-        w2_bf16 = {}
-
-        def gather(dst, window, fields):
-            for f in fields:
-                nc.vector.tensor_copy(
-                    dst[:, f * S : (f + 1) * S], window.indirect(offsets[:, f * S // 16 : (f + 1) * S // 16])
-                )
-
-        def interleave(copy, h, a, cols, dst=None):
-            copy(
-                (w2_bf16[h, a][:, cols, :] if dst is None else dst).rearrange("p (c i) j -> p c j i", i=4),
-                w2_raw[h, a][:, :, cols].rearrange("p j (c i) -> p c j i", i=4),
-            )
-
-        def quantize(h, a, cols=slice(0, HALF), src=None):
-            nc.vector.quantize_mx(
-                out=w2_codes[:, h, a, cols].bitcast(FP8X4),
-                scales=w2_scales[h, a][:, cols],
-                in_=(w2_bf16[h, a][:] if src is None else src).rearrange("p n j -> p (n j)"),
-            )
-
-        picked_scales = keep.tile([P, FIELDS * S], U8, name="picked_scales", align_bytes=64)
-        gather(picked_scales, tab_scales[:].bitcast(U8), (0, 2, 1))
-        gather(picked_words[0], tab_words[0][:].bitcast(U32), (0, 2, 1))
-        moved_rows = P - QUAD + ROWS
-        nc.sync.dma_start(
-            shifted_scales[0:moved_rows, :], picked_scales[ROWS : ROWS + moved_rows, 0:S].bitcast(I32)
-        )
         for h in range(HALVES):
             raw = reuse.tile([P, PACK, HALF], F32, name=f"w2_raw1_{h}", align_bytes=64, offset=(12 + 4 * h) * KIB + 64)
             w2_raw[h, 1] = raw[:]
@@ -142,80 +142,66 @@ def tile_list_tabfield_tm_gelu_kernel(
         for h, start in enumerate((20 * KIB + 64, 23 * KIB)):
             w1_codes.append(reuse.tile([P, PASSES, HALF], I32, name=f"w1_codes{h}", align_bytes=64, offset=start))
             nc.sync.dma_start(w1_codes[h][:], w1_rows[:, :, h * HALF : (h + 1) * HALF])
-        w2_bf16[0, 0] = reuse.tile([P, HALF, PACK], BF16, name="w2_bf16_00", align_bytes=64, offset=2 * KIB)
-        w2_bf16[1, 0] = reuse.tile([P, HALF, PACK], BF16, name="w2_bf16_10", align_bytes=64, offset=0)
-        interleave(nc.scalar.copy, 0, 0, slice(0, HALF))
-        interleave(nc.vector.tensor_copy, 1, 0, slice(0, HALF))
-        quantize(1, 0)
+        interleave(nc.vector.tensor_copy, 0, 0, slice(0, HALF))
+        interleave(nc.scalar.copy, 1, 0, slice(0, HALF))
         quantize(0, 0)
-        picked_words.append(reuse.tile([P, FIELDS * S], U32, name="picked_words1", align_bytes=64, offset=1 * KIB))
-        gather(picked_words[1], tab_words[1][:].bitcast(U32), (0, 2, 1))
-        for h in range(HALVES):
-            w2_bf16[h, 1] = keep.tile([P, HALF, PACK], BF16, name=f"w2_bf16_{h}1", align_bytes=64)
-        interleave(nc.scalar.copy, 0, 1, slice(0, HALF - VECTOR_COLS_FIRST))
-        interleave(nc.vector.tensor_copy, 0, 1, slice(HALF - VECTOR_COLS_FIRST, HALF))
-        quantize(0, 1)
-        interleave(nc.vector.tensor_copy, 1, 1, slice(0, VECTOR_COLS))
-        interleave(nc.scalar.copy, 1, 1, slice(VECTOR_COLS, HALF))
-        quantize(1, 1)
+        quantize(1, 0)
+        for h, vector_cols in enumerate(VECTOR_COLS):
+            interleave(nc.scalar.copy, h, 1, slice(0, HALF - vector_cols))
+            interleave(nc.vector.tensor_copy, h, 1, slice(HALF - vector_cols, HALF))
+            quantize(h, 1)
 
-        w0_scale_bytes = w_planes[:, 0, :, :].bitcast(U8)
-        w1_scale_bytes = w_planes[:, 1, :, :].bitcast(U8)
+        plane_bytes = planes[:].bitcast(U8)
+        w1_scale_bytes = w1_planes[ROWS:P, :, :].bitcast(U8)
         w0_bytes = w0_codes[:].bitcast(U8)
         acc = [
             [psum.tile([P, HALF], F32, name=f"acc{h}{tt}") for tt in range(TOKEN_TILES)] for h in range(HALVES)
         ]
 
         def table_pass(h, tt, f, a, cols, rhs, rhs_scale, start, stop):
-            tokens = slice(f * S + tt * P, f * S + (tt + 1) * P)
-            if (f, a) == (0, 1):
-                table_scale = shifted_scales[:].bitcast(U8)[:, tokens]
-            else:
-                table_scale = picked_scales[ROWS * a : P, tokens]
+            first = f * S + tt * P
             nc.tensor.matmul_mx(
                 out=acc[h][tt][:, cols],
-                lhsT=picked_words[a][:, tokens].bitcast(FP8X4),
-                lhsT_scale=table_scale,
+                lhsT=picked_words[a][:, first : first + P].bitcast(FP8X4),
+                lhsT_scale=plane_bytes[:, a, M + first : M + first + P],
                 rhs=rhs,
                 rhs_scale=rhs_scale,
                 start=start,
                 stop=stop,
             )
 
-        def w2_passes(h, a, start):
+        def w2_passes(h, a):
             for tt in range(TOKEN_TILES):
                 table_pass(
-                    h, tt, 2, a, slice(0, HALF), w2_codes[:, h, a, :].bitcast(FP8X4), w2_scales[h, a][:], start, False
+                    h, tt, 2, a, slice(0, HALF), w2_codes[:, h, a, :].bitcast(FP8X4), w2_scales[h, a][:], False, False
                 )
 
-        def w0_passes(h, a, opens=False):
+        def w0_passes(h, a):
             for tt in range(TOKEN_TILES):
                 for c0 in range(0, HALF, P):
                     n0 = h * HALF + c0
                     table_pass(
                         h, tt, 0, a, slice(c0, c0 + P),
                         w0_bytes[:, a, 2 * n0 : 2 * (n0 + P)].bitcast(FP4X4),
-                        w0_scale_bytes[:, a, n0 : n0 + P], opens and c0 == 0, False,
+                        plane_bytes[:, a, n0 : n0 + P], a == 0 and c0 == 0, False,
                     )
 
         def w1_passes(h):
-            cols = slice(h * HALF, (h + 1) * HALF)
             for tt in range(TOKEN_TILES):
                 for a in range(PASSES):
                     table_pass(
                         h, tt, 1, a, slice(0, HALF), w1_codes[h][:, a, :].bitcast(FP8X4),
-                        w1_scale_bytes[:, a, cols], False, a == PASSES - 1,
+                        w1_scale_bytes[:, a, h * HALF : (h + 1) * HALF], False, a == PASSES - 1,
                     )
 
-        w2_passes(1, 0, True)
-        w2_passes(0, 0, True)
-        for a in range(PASSES):
-            for h in range(HALVES):
-                w0_passes(h, a)
-        w2_passes(0, 1, False)
-        w1_passes(0)
-        w2_passes(1, 1, False)
-        w1_passes(1)
+        for h in range(HALVES):
+            w0_passes(h, 0)
+        for h in range(HALVES):
+            w2_passes(h, 0)
+            w0_passes(h, 1)
+        for h in range(HALVES):
+            w2_passes(h, 1)
+            w1_passes(h)
 
         summed = [keep.tile([P, TOKEN_TILES, HALF], F32, name=f"summed{h}") for h in range(HALVES)]
         result = [keep.tile([P, TOKEN_TILES, HALF], F32, name=f"result{h}") for h in range(HALVES)]

@@ -26,9 +26,10 @@ TOKEN_TILES = S // P
 QUAD = 32
 ROWS = 4
 KIB = 1024
-LIVE = P - PASSES * 16
+SPREAD = 4
 PLANE = M + FIELDS * S
-VECTOR_COLS = (120, 144)
+VECTOR_COLS = 152
+LAST_SCALAR_COLS = 160
 
 
 def tile_list_tabfield_tm_gelu_kernel(
@@ -43,7 +44,8 @@ def tile_list_tabfield_tm_gelu_kernel(
         scale_window = keep.tile([P, T // 4], I32, name="scale_window", align_bytes=64)
         staged = keep.tile([P, PLANE // 4], I32, name="staged", align_bytes=64)
         planes = keep.tile([P, PASSES, PLANE // 4], I32, name="planes", align_bytes=64)
-        nc.vector.memset(scale_window[0:LIVE, :], 0)
+        nc.vector.memset(scale_window[:, 0 : T // 8], 0)
+        nc.gpsimd.memset(scale_window[:, T // 8 : T // 4], 0)
         w1_planes = keep.tile([P, PASSES, M // 4], I32, name="w1_planes", align_bytes=64)
         nc.vector.memset(w1_planes[:], 0)
         nc.vector.memset(planes[:], 0)
@@ -68,16 +70,16 @@ def tile_list_tabfield_tm_gelu_kernel(
             nc.sync.dma_start(dst, rows.rearrange("(p j) n -> p j n", j=PACK))
 
         nc.sync.dma_start(offsets[:], offs)
-        nc.sync.dma_start(
-            scale_window[LIVE:P, :], tab[:, K_PASS * T :].rearrange("a (q t) -> q a t", t=T).bitcast(I32)
-        )
-        nc.sync.dma_start(staged[LIVE:P, 0 : M // 4], w0_scales.rearrange("a q n -> q a n").bitcast(I32))
+        nc.sync.dma_start(staged[0:P:SPREAD, 0 : M // 4], w0_scales.rearrange("a q n -> q a n").bitcast(I32))
         nc.sync.dma_start(b_cols[:], b.rearrange("(p c) -> p c", c=PACK))
+        nc.sync.dma_start(w0_codes[:], w0_words.rearrange("a p c -> p a c").bitcast(I32))
+        nc.sync.dma_start(
+            scale_window[0:P:SPREAD, :], tab[:, K_PASS * T :].rearrange("a (q t) -> q a t", t=T).bitcast(I32)
+        )
         for a in range(PASSES):
             nc.sync.dma_start(
                 tab_words[a][:], tab[a, 0 : K_PASS * T].rearrange("(p w) -> p w", p=P).bitcast(I32)
             )
-        nc.sync.dma_start(w0_codes[:], w0_words.rearrange("a p c -> p a c").bitcast(I32))
         load_w2(w2_raw0[:], 0, slice(0, M))
 
         picked_words = [keep.tile([P, FIELDS * S], U32, name=f"picked_words{a}", align_bytes=64) for a in range(PASSES)]
@@ -113,16 +115,14 @@ def tile_list_tabfield_tm_gelu_kernel(
             )
 
         gather(picked_scales, scale_window[:].bitcast(U8), 0, FIELDS)
-        nc.vector.tensor_copy(staged[LIVE:P, M // 4 : PLANE // 4], picked_scales[LIVE:P, :].bitcast(I32))
+        nc.vector.tensor_copy(staged[:, M // 4 : PLANE // 4], picked_scales[:].bitcast(I32))
         for quad in (0, 2, 1, 3):
-            first = LIVE + PASSES * ROWS * quad
             nc.scalar.dma_start(
                 planes[QUAD * quad : QUAD * quad + ROWS, :, :].rearrange("p a n -> p (a n)"),
-                staged[first : first + PASSES * ROWS, :],
+                staged[QUAD * quad : QUAD * (quad + 1) : SPREAD, :],
             )
-        gather(picked_words[0], tab_words[0][:].bitcast(U32), 0, FIELDS)
-        gather(picked_words[1], tab_words[1][:].bitcast(U32), 0, 1)
-        gather(picked_words[1], tab_words[1][:].bitcast(U32), 1, FIELDS)
+        for a in range(PASSES):
+            gather(picked_words[a], tab_words[a][:].bitcast(U32), 0, FIELDS)
 
         identity = keep.tile([P, P], F32, name="identity")
         make_identity(nc, identity[:])
@@ -133,22 +133,34 @@ def tile_list_tabfield_tm_gelu_kernel(
         nc.scalar.copy(bias[:], bias_bank[:].rearrange("j c p -> j p c"))
         bias_row = bias[:].rearrange("j p c -> j (p c)")
 
-        for h in range(HALVES):
-            raw = reuse.tile([P, PACK, HALF], F32, name=f"w2_raw1_{h}", align_bytes=64, offset=(12 + 4 * h) * KIB + 64)
-            w2_raw[h, 1] = raw[:]
-            load_w2(raw[:], 1, slice(h * HALF, (h + 1) * HALF))
-        w1_codes = []
+        w2_last = w2[K_PASS:K, :].rearrange("(p u j) n -> p u j n", u=2, j=2)
+        w2_pairs = []
+        for u in range(2):
+            w2_pairs.append(reuse.tile([P, 2, M], F32, name=f"w2_pair{u}", align_bytes=64, offset=(12 + 4 * u) * KIB + 64))
+            nc.sync.dma_start(w2_pairs[u][:], w2_last[:, u, :, :])
+        w1_codes = {}
         w1_rows = w1_words.rearrange("a p n i -> p a (n i)").bitcast(I32)
-        for h, start in enumerate((20 * KIB + 64, 23 * KIB)):
-            w1_codes.append(reuse.tile([P, PASSES, HALF], I32, name=f"w1_codes{h}", align_bytes=64, offset=start))
-            nc.sync.dma_start(w1_codes[h][:], w1_rows[:, :, h * HALF : (h + 1) * HALF])
-        interleave(nc.vector.tensor_copy, 0, 0, slice(0, HALF))
-        interleave(nc.scalar.copy, 1, 0, slice(0, HALF))
-        quantize(0, 0)
-        quantize(1, 0)
-        for h, vector_cols in enumerate(VECTOR_COLS):
-            interleave(nc.scalar.copy, h, 1, slice(0, HALF - vector_cols))
-            interleave(nc.vector.tensor_copy, h, 1, slice(HALF - vector_cols, HALF))
+        for h in range(HALVES):
+            for a in range(PASSES):
+                start = (20 + PASSES * h + a) * KIB + 64
+                w1_codes[h, a] = reuse.tile([P, HALF], I32, name=f"w1_codes{h}{a}", align_bytes=64, offset=start)
+                nc.sync.dma_start(w1_codes[h, a][:], w1_rows[:, a, h * HALF : (h + 1) * HALF])
+        for h in range(HALVES):
+            interleave(nc.scalar.copy, h, 0, slice(0, HALF - VECTOR_COLS))
+            interleave(nc.vector.tensor_copy, h, 0, slice(HALF - VECTOR_COLS, HALF))
+        for h in range(HALVES):
+            quantize(h, 0)
+        for copy, u, h, first, last in (
+            (nc.vector.tensor_copy, 0, 0, 0, HALF),
+            (nc.scalar.copy, 0, 1, 0, HALF - 32), (nc.vector.tensor_copy, 0, 1, HALF - 32, HALF),
+            (nc.vector.tensor_copy, 1, 0, 0, HALF),
+            (nc.scalar.copy, 1, 1, 0, LAST_SCALAR_COLS), (nc.vector.tensor_copy, 1, 1, LAST_SCALAR_COLS, HALF),
+        ):
+            copy(
+                w2_bf16[h, 1][:, first:last, 2 * u : 2 * u + 2].rearrange("p (c i) j -> p c j i", i=4),
+                w2_pairs[u][:, :, h * HALF + first : h * HALF + last].rearrange("p j (c i) -> p c j i", i=4),
+            )
+        for h in range(HALVES):
             quantize(h, 1)
 
         plane_bytes = planes[:].bitcast(U8)
@@ -170,11 +182,11 @@ def tile_list_tabfield_tm_gelu_kernel(
                 stop=stop,
             )
 
-        def w2_passes(h, a):
-            for tt in range(TOKEN_TILES):
-                table_pass(
-                    h, tt, 2, a, slice(0, HALF), w2_codes[:, h, a, :].bitcast(FP8X4), w2_scales[h, a][:], False, False
-                )
+        def w2_pass(h, tt, a):
+            table_pass(
+                h, tt, 2, a, slice(0, HALF), w2_codes[:, h, a, :].bitcast(FP8X4), w2_scales[h, a][:],
+                False, (h, a) == (0, PASSES - 1),
+            )
 
         def w0_passes(h, a):
             for tt in range(TOKEN_TILES):
@@ -186,32 +198,40 @@ def tile_list_tabfield_tm_gelu_kernel(
                         plane_bytes[:, a, n0 : n0 + P], a == 0 and c0 == 0, False,
                     )
 
-        def w1_passes(h):
-            for tt in range(TOKEN_TILES):
-                for a in range(PASSES):
-                    table_pass(
-                        h, tt, 1, a, slice(0, HALF), w1_codes[h][:, a, :].bitcast(FP8X4),
-                        w1_scale_bytes[:, a, h * HALF : (h + 1) * HALF], False, a == PASSES - 1,
-                    )
+        def w1_pass(h, tt, a):
+            table_pass(
+                h, tt, 1, a, slice(0, HALF), w1_codes[h, a][:].bitcast(FP8X4),
+                w1_scale_bytes[:, a, h * HALF : (h + 1) * HALF], False, (h, a) == (1, PASSES - 1),
+            )
 
-        for h in range(HALVES):
-            w0_passes(h, 0)
-        for h in range(HALVES):
-            w2_passes(h, 0)
-            w0_passes(h, 1)
-        for h in range(HALVES):
-            w2_passes(h, 1)
-            w1_passes(h)
+        for a in range(PASSES):
+            for h in range(HALVES):
+                w0_passes(h, a)
+        for one_pass, h, a in (
+            (w2_pass, 0, 0), (w2_pass, 1, 0),
+            (w1_pass, 0, 0), (w1_pass, 0, 1), (w2_pass, 0, 1), (w1_pass, 1, 0), (w2_pass, 1, 1), (w1_pass, 1, 1),
+        ):
+            for tt in range(TOKEN_TILES):
+                one_pass(h, tt, a)
 
         summed = [keep.tile([P, TOKEN_TILES, HALF], F32, name=f"summed{h}") for h in range(HALVES)]
         result = [keep.tile([P, TOKEN_TILES, HALF], F32, name=f"result{h}") for h in range(HALVES)]
         out_view = out.rearrange("(tt p) n -> p tt n", p=P)
-        for h in range(HALVES):
-            cols = slice(h * HALF, (h + 1) * HALF)
-            for tt in range(TOKEN_TILES):
-                nc.vector.tensor_tensor(summed[h][:, tt, :], acc[h][tt][:], bias_row[:, cols], mybir.AluOpType.add)
-                nc.scalar.activation(result[h][:, tt, :], summed[h][:, tt, :], mybir.ActivationFunctionType.Gelu_apprx_tanh)
-                if h == HALVES - 1:
-                    nc.sync.dma_start(out_view[:, tt, cols], result[h][:, tt, :])
-            if h < HALVES - 1:
-                nc.sync.dma_start(out_view[:, :, cols], result[h][:])
+
+        def finish(h, tt, first, last):
+            nc.vector.tensor_tensor(
+                summed[h][:, tt, first:last], acc[h][tt][:, first:last],
+                bias_row[:, h * HALF + first : h * HALF + last], mybir.AluOpType.add,
+            )
+            nc.scalar.activation(
+                result[h][:, tt, first:last], summed[h][:, tt, first:last],
+                mybir.ActivationFunctionType.Gelu_apprx_tanh,
+            )
+
+        for tt in range(TOKEN_TILES):
+            finish(0, tt, 0, HALF)
+        nc.sync.dma_start(out_view[:, :, 0:HALF], result[0][:])
+        finish(1, 0, 0, HALF)
+        nc.sync.dma_start(out_view[:, 0, HALF:M], result[1][:, 0, :])
+        finish(1, 1, 0, HALF)
+        nc.sync.dma_start(out_view[:, 1, HALF:M], result[1][:, 1, :])

@@ -69,10 +69,10 @@ def tile_list_tabfield_tm_gelu_kernel(
             rows = w2[a * K_PASS : (a + 1) * K_PASS, cols]
             nc.sync.dma_start(dst, rows.rearrange("(p j) n -> p j n", j=PACK))
 
+        nc.sync.dma_start(w0_codes[:], w0_words.rearrange("a p c -> p a c").bitcast(I32))
         nc.sync.dma_start(offsets[:], offs)
         nc.sync.dma_start(staged[0:P:SPREAD, 0 : M // 4], w0_scales.rearrange("a q n -> q a n").bitcast(I32))
         nc.sync.dma_start(b_cols[:], b.rearrange("(p c) -> p c", c=PACK))
-        nc.sync.dma_start(w0_codes[:], w0_words.rearrange("a p c -> p a c").bitcast(I32))
         nc.sync.dma_start(
             scale_window[0:P:SPREAD, :], tab[:, K_PASS * T :].rearrange("a (q t) -> q a t", t=T).bitcast(I32)
         )
@@ -228,10 +228,6 @@ def tile_list_tabfield_tm_gelu_kernel(
                 mybir.ActivationFunctionType.Gelu_apprx_tanh,
             )
 
-        for tt in range(TOKEN_TILES):
-            finish(0, tt, 0, HALF)
-        nc.sync.dma_start(out_view[:, :, 0:HALF], result[0][:])
-        finish(1, 0, 0, HALF)
-        nc.sync.dma_start(out_view[:, 0, HALF:M], result[1][:, 0, :])
-        finish(1, 1, 0, HALF)
-        nc.sync.dma_start(out_view[:, 1, HALF:M], result[1][:, 1, :])
+        for h, tt, first, last in ((0, 0, 0, HALF), (0, 1, 0, HALF), (1, 0, 0, HALF), (1, 1, 0, P), (1, 1, P, HALF)):
+            finish(h, tt, first, last)
+            nc.sync.dma_start(out_view[:, tt, h * HALF + first : h * HALF + last], result[h][:, tt, first:last])

@@ -41,6 +41,10 @@ def tile_list_tabfield_tm_gelu_kernel(
         reuse = ctx.enter_context(tc.tile_pool(name="reuse", bufs=1))
         psum = ctx.enter_context(tc.psum_pool(name="psum", bufs=1))
 
+        warm = keep.tile([P, 2], F32, name="warm")
+        nc.vector.memset(warm[:, 0:1], 0.0)
+        nc.scalar.activation(warm[:, 1:2], warm[:, 0:1], mybir.ActivationFunctionType.Gelu_apprx_tanh)
+
         scale_window = keep.tile([P, T // 4], I32, name="scale_window", align_bytes=64)
         staged = keep.tile([P, PLANE // 4], I32, name="staged", align_bytes=64)
         planes = keep.tile([P, PASSES, PLANE // 4], I32, name="planes", align_bytes=64)

@@ -199,7 +199,7 @@ def tile_list_tabfield_tm_gelu_kernel(
                     table_pass(
                         h, tt, 0, a, slice(c0, c0 + P),
                         w0_bytes[:, a, 2 * n0 : 2 * (n0 + P)].bitcast(FP4X4),
-                        plane_bytes[:, a, n0 : n0 + P], a == 0 and c0 == 0, False,
+                        plane_bytes[:, a, n0 : n0 + P], a == PASSES - 1 and c0 == 0, False,
                     )
 
         def w1_pass(h, tt, a):
@@ -208,7 +208,7 @@ def tile_list_tabfield_tm_gelu_kernel(
                 w1_scale_bytes[:, a, h * HALF : (h + 1) * HALF], False, (h, a) == (1, PASSES - 1),
             )
 
-        for a in range(PASSES):
+        for a in reversed(range(PASSES)):
             for h in range(HALVES):
                 w0_passes(h, a)
         for one_pass, h, a in (

@@ -27,7 +27,8 @@ QUAD = 32
 ROWS = 4
 KIB = 1024
 SPREAD = 4
-PLANE = M + FIELDS * S
+PLANE = M + S
+LATER = (FIELDS - 1) * S
 VECTOR_COLS = 152
 LAST_SCALAR_COLS = 160
 
@@ -53,6 +54,8 @@ def tile_list_tabfield_tm_gelu_kernel(
         w1_planes = keep.tile([P, PASSES, M // 4], I32, name="w1_planes", align_bytes=64)
         nc.vector.memset(w1_planes[:], 0)
         nc.vector.memset(planes[:], 0)
+        later_planes = keep.tile([P, PASSES, LATER // 4], I32, name="later_planes", align_bytes=64)
+        nc.vector.memset(later_planes[:], 0)
         for quad in range(P // QUAD):
             nc.gpsimd.dma_start(
                 w1_planes[QUAD * quad + ROWS : QUAD * quad + 2 * ROWS, :, :],
@@ -119,11 +122,17 @@ def tile_list_tabfield_tm_gelu_kernel(
             )
 
         gather(picked_scales, scale_window[:].bitcast(U8), 0, FIELDS)
-        nc.vector.tensor_copy(staged[:, M // 4 : PLANE // 4], picked_scales[:].bitcast(I32))
+        picked_scale_words = picked_scales[:].bitcast(I32)
+        nc.vector.tensor_copy(staged[:, M // 4 : PLANE // 4], picked_scale_words[:, 0 : S // 4])
         for quad in (0, 2, 1, 3):
             nc.scalar.dma_start(
                 planes[QUAD * quad : QUAD * quad + ROWS, :, :].rearrange("p a n -> p (a n)"),
                 staged[QUAD * quad : QUAD * (quad + 1) : SPREAD, :],
+            )
+        for quad in (0, 2, 1, 3):
+            nc.gpsimd.dma_start(
+                later_planes[QUAD * quad + 2 * ROWS : QUAD * quad + 3 * ROWS, :, :].rearrange("p a n -> p (a n)"),
+                picked_scale_words[QUAD * quad : QUAD * (quad + 1) : SPREAD, S // 4 : FIELDS * S // 4],
             )
         for a in range(PASSES):
             gather(picked_words[a], tab_words[a][:].bitcast(U32), 0, FIELDS)
@@ -169,6 +178,7 @@ def tile_list_tabfield_tm_gelu_kernel(
 
         plane_bytes = planes[:].bitcast(U8)
         w1_scale_bytes = w1_planes[ROWS:P, :, :].bitcast(U8)
+        later_bytes = later_planes[2 * ROWS : P, :, :].bitcast(U8)
         w0_bytes = w0_codes[:].bitcast(U8)
         acc = [
             [psum.tile([P, HALF], F32, name=f"acc{h}{tt}") for tt in range(TOKEN_TILES)] for h in range(HALVES)
@@ -179,7 +189,9 @@ def tile_list_tabfield_tm_gelu_kernel(
             nc.tensor.matmul_mx(
                 out=acc[h][tt][:, cols],
                 lhsT=picked_words[a][:, first : first + P].bitcast(FP8X4),
-                lhsT_scale=plane_bytes[:, a, M + first : M + first + P],
+                lhsT_scale=(
+                    plane_bytes[:, a, M + first : M + first + P] if f == 0 else later_bytes[:, a, first - S : first - S + P]
+                ),
                 rhs=rhs,
                 rhs_scale=rhs_scale,
                 start=start,

@@ -15,6 +15,7 @@ U16 = mybir.dt.uint16
 U8 = mybir.dt.uint8
 FP8X4 = mybir.dt.float8_e4m3fn_x4
 FP4X4 = mybir.dt.float4_e2m1fn_x4
+GELU = mybir.ActivationFunctionType.Gelu_apprx_tanh
 
 P = 128
 PACK = 4
@@ -30,7 +31,6 @@ SPREAD = 4
 PLANE = M + S
 LATER = (FIELDS - 1) * S
 VECTOR_COLS = 152
-LAST_SCALAR_COLS = 160
 
 
 def tile_list_tabfield_tm_gelu_kernel(
@@ -42,10 +42,6 @@ def tile_list_tabfield_tm_gelu_kernel(
         reuse = ctx.enter_context(tc.tile_pool(name="reuse", bufs=1))
         psum = ctx.enter_context(tc.psum_pool(name="psum", bufs=1))
 
-        warm = keep.tile([P, 2], F32, name="warm")
-        nc.vector.memset(warm[:, 0:1], 0.0)
-        nc.scalar.activation(warm[:, 1:2], warm[:, 0:1], mybir.ActivationFunctionType.Gelu_apprx_tanh)
-
         scale_window = keep.tile([P, T // 4], I32, name="scale_window", align_bytes=64)
         staged = keep.tile([P, PLANE // 4], I32, name="staged", align_bytes=64)
         planes = keep.tile([P, PASSES, PLANE // 4], I32, name="planes", align_bytes=64)
@@ -53,6 +49,9 @@ def tile_list_tabfield_tm_gelu_kernel(
         nc.gpsimd.memset(scale_window[:, T // 8 : T // 4], 0)
         w1_planes = keep.tile([P, PASSES, M // 4], I32, name="w1_planes", align_bytes=64)
         nc.vector.memset(w1_planes[:], 0)
+        warm = keep.tile([P, 2], F32, name="warm")
+        nc.vector.memset(warm[:, 0:1], 0.0)
+        nc.scalar.activation(warm[:, 1:2], warm[:, 0:1], GELU)
         nc.vector.memset(planes[:], 0)
         later_planes = keep.tile([P, PASSES, LATER // 4], I32, name="later_planes", align_bytes=64)
         nc.vector.memset(later_planes[:], 0)
@@ -70,11 +69,6 @@ def tile_list_tabfield_tm_gelu_kernel(
         ]
         w0_codes = keep.tile([P, PASSES, 2 * M // 4], I32, name="w0_codes", align_bytes=64)
         w2_raw0 = keep.tile([P, PACK, M], F32, name="w2_raw0", align_bytes=64)
-        w2_raw = {(h, 0): w2_raw0[:, :, h * HALF : (h + 1) * HALF] for h in range(HALVES)}
-
-        def load_w2(dst, a, cols):
-            rows = w2[a * K_PASS : (a + 1) * K_PASS, cols]
-            nc.sync.dma_start(dst, rows.rearrange("(p j) n -> p j n", j=PACK))
 
         nc.sync.dma_start(w0_codes[:], w0_words.rearrange("a p c -> p a c").bitcast(I32))
         nc.sync.dma_start(offsets[:], offs)
@@ -87,10 +81,11 @@ def tile_list_tabfield_tm_gelu_kernel(
             nc.sync.dma_start(
                 tab_words[a][:], tab[a, 0 : K_PASS * T].rearrange("(p w) -> p w", p=P).bitcast(I32)
             )
-        load_w2(w2_raw0[:], 0, slice(0, M))
+        nc.sync.dma_start(w2_raw0[:], w2[0:K_PASS, :].rearrange("(p j) n -> p j n", j=PACK))
 
         picked_words = [keep.tile([P, FIELDS * S], U32, name=f"picked_words{a}", align_bytes=64) for a in range(PASSES)]
-        picked_scales = keep.tile([P, FIELDS * S], U8, name="picked_scales", align_bytes=64)
+        first_scales = keep.tile([P, S], U8, name="first_scales", align_bytes=64)
+        later_scales = keep.tile([P, LATER], U8, name="later_scales", align_bytes=64)
         w2_codes = keep.tile([P, HALVES, PASSES, HALF], U32, name="w2_codes", align_bytes=64)
         w2_scales = {
             (h, a): keep.tile([P, HALF], U8, name=f"w2_scales_{h}{a}", align_bytes=64)
@@ -104,14 +99,12 @@ def tile_list_tabfield_tm_gelu_kernel(
         }
 
         def gather(dst, window, first, last):
-            nc.vector.tensor_copy(
-                dst[:, first * S : last * S], window.indirect(offsets[:, first * S // 16 : last * S // 16])
-            )
+            nc.vector.tensor_copy(dst[:], window.indirect(offsets[:, first * S // 16 : last * S // 16]))
 
-        def interleave(copy, h, a, cols):
+        def interleave(copy, h, first, last):
             copy(
-                w2_bf16[h, a][:, cols, :].rearrange("p (c i) j -> p c j i", i=4),
-                w2_raw[h, a][:, :, cols].rearrange("p j (c i) -> p c j i", i=4),
+                w2_bf16[h, 0][:, first:last, :].rearrange("p (c i) j -> p c j i", i=4),
+                w2_raw0[:, :, h * HALF + first : h * HALF + last].rearrange("p j (c i) -> p c j i", i=4),
             )
 
         def quantize(h, a):
@@ -121,9 +114,9 @@ def tile_list_tabfield_tm_gelu_kernel(
                 in_=w2_bf16[h, a][:].rearrange("p n j -> p (n j)"),
             )
 
-        gather(picked_scales, scale_window[:].bitcast(U8), 0, FIELDS)
-        picked_scale_words = picked_scales[:].bitcast(I32)
-        nc.vector.tensor_copy(staged[:, M // 4 : PLANE // 4], picked_scale_words[:, 0 : S // 4])
+        gather(later_scales, scale_window[:].bitcast(U8), 1, FIELDS)
+        gather(first_scales, scale_window[:].bitcast(U8), 0, 1)
+        nc.vector.tensor_copy(staged[:, M // 4 : PLANE // 4], first_scales[:].bitcast(I32))
         for quad in (0, 2, 1, 3):
             nc.scalar.dma_start(
                 planes[QUAD * quad : QUAD * quad + ROWS, :, :].rearrange("p a n -> p (a n)"),
@@ -132,7 +125,7 @@ def tile_list_tabfield_tm_gelu_kernel(
         for quad in (0, 2, 1, 3):
             nc.gpsimd.dma_start(
                 later_planes[QUAD * quad + 2 * ROWS : QUAD * quad + 3 * ROWS, :, :].rearrange("p a n -> p (a n)"),
-                picked_scale_words[QUAD * quad : QUAD * (quad + 1) : SPREAD, S // 4 : FIELDS * S // 4],
+                later_scales[QUAD * quad : QUAD * (quad + 1) : SPREAD, :].bitcast(I32),
             )
         for a in range(PASSES):
             gather(picked_words[a], tab_words[a][:].bitcast(U32), 0, FIELDS)
@@ -147,10 +140,13 @@ def tile_list_tabfield_tm_gelu_kernel(
         bias_row = bias[:].rearrange("j p c -> j (p c)")
 
         w2_last = w2[K_PASS:K, :].rearrange("(p u j) n -> p u j n", u=2, j=2)
-        w2_pairs = []
-        for u in range(2):
-            w2_pairs.append(reuse.tile([P, 2, M], F32, name=f"w2_pair{u}", align_bytes=64, offset=(12 + 4 * u) * KIB + 64))
-            nc.sync.dma_start(w2_pairs[u][:], w2_last[:, u, :, :])
+        first_pair = reuse.tile([P, 2, M], F32, name="first_pair", align_bytes=64, offset=12 * KIB + 64)
+        nc.sync.dma_start(first_pair[:], w2_last[:, 0, :, :])
+        w2_pairs = {(0, h): first_pair[:, :, h * HALF : (h + 1) * HALF] for h in range(HALVES)}
+        second_pair = reuse.tile([P, 2, M], F32, name="second_pair", align_bytes=64, offset=16 * KIB + 64)
+        nc.sync.dma_start(second_pair[:], w2_last[:, 1, :, :])
+        for h in range(HALVES):
+            w2_pairs[1, h] = second_pair[:, :, h * HALF : (h + 1) * HALF]
         w1_codes = {}
         w1_rows = w1_words.rearrange("a p n i -> p a (n i)").bitcast(I32)
         for h in range(HALVES):
@@ -159,20 +155,23 @@ def tile_list_tabfield_tm_gelu_kernel(
                 w1_codes[h, a] = reuse.tile([P, HALF], I32, name=f"w1_codes{h}{a}", align_bytes=64, offset=start)
                 nc.sync.dma_start(w1_codes[h, a][:], w1_rows[:, a, h * HALF : (h + 1) * HALF])
         for h in range(HALVES):
-            interleave(nc.scalar.copy, h, 0, slice(0, HALF - VECTOR_COLS))
-            interleave(nc.vector.tensor_copy, h, 0, slice(HALF - VECTOR_COLS, HALF))
+            interleave(nc.scalar.copy, h, 0, HALF - VECTOR_COLS)
+            interleave(nc.vector.tensor_copy, h, HALF - VECTOR_COLS, HALF)
         for h in range(HALVES):
             quantize(h, 0)
-        for copy, u, h, first, last in (
-            (nc.vector.tensor_copy, 0, 0, 0, HALF),
-            (nc.scalar.copy, 0, 1, 0, HALF - 32), (nc.vector.tensor_copy, 0, 1, HALF - 32, HALF),
-            (nc.vector.tensor_copy, 1, 0, 0, HALF),
-            (nc.scalar.copy, 1, 1, 0, LAST_SCALAR_COLS), (nc.vector.tensor_copy, 1, 1, LAST_SCALAR_COLS, HALF),
-        ):
+
+        def interleave_pair(copy, u, h, first, last):
             copy(
                 w2_bf16[h, 1][:, first:last, 2 * u : 2 * u + 2].rearrange("p (c i) j -> p c j i", i=4),
-                w2_pairs[u][:, :, h * HALF + first : h * HALF + last].rearrange("p j (c i) -> p c j i", i=4),
+                w2_pairs[u, h][:, :, first:last].rearrange("p j (c i) -> p c j i", i=4),
             )
+
+        interleave_pair(nc.vector.tensor_copy, 0, 0, 0, 256)
+        interleave_pair(nc.scalar.copy, 0, 1, 0, 192)
+        interleave_pair(nc.vector.tensor_copy, 0, 1, 192, 256)
+        interleave_pair(nc.vector.tensor_copy, 1, 0, 0, 256)
+        interleave_pair(nc.scalar.copy, 1, 1, 0, 144)
+        interleave_pair(nc.vector.tensor_copy, 1, 1, 144, 256)
         for h in range(HALVES):
             quantize(h, 1)
 
@@ -198,12 +197,6 @@ def tile_list_tabfield_tm_gelu_kernel(
                 stop=stop,
             )
 
-        def w2_pass(h, tt, a):
-            table_pass(
-                h, tt, 2, a, slice(0, HALF), w2_codes[:, h, a, :].bitcast(FP8X4), w2_scales[h, a][:],
-                False, (h, a) == (0, PASSES - 1),
-            )
-
         def w0_passes(h, a):
             for tt in range(TOKEN_TILES):
                 for c0 in range(0, HALF, P):
@@ -214,21 +207,29 @@ def tile_list_tabfield_tm_gelu_kernel(
                         plane_bytes[:, a, n0 : n0 + P], a == PASSES - 1 and c0 == 0, False,
                     )
 
-        def w1_pass(h, tt, a):
+        def w1_pass(h, tt, a, stop):
             table_pass(
                 h, tt, 1, a, slice(0, HALF), w1_codes[h, a][:].bitcast(FP8X4),
-                w1_scale_bytes[:, a, h * HALF : (h + 1) * HALF], False, (h, a) == (1, PASSES - 1),
+                w1_scale_bytes[:, a, h * HALF : (h + 1) * HALF], False, stop,
+            )
+
+        def w2_pass(h, tt, a, stop):
+            table_pass(
+                h, tt, 2, a, slice(0, HALF), w2_codes[:, h, a, :].bitcast(FP8X4), w2_scales[h, a][:], False, stop,
             )
 
         for a in reversed(range(PASSES)):
             for h in range(HALVES):
                 w0_passes(h, a)
-        for one_pass, h, a in (
-            (w2_pass, 0, 0), (w2_pass, 1, 0),
-            (w1_pass, 0, 0), (w1_pass, 0, 1), (w2_pass, 0, 1), (w1_pass, 1, 0), (w2_pass, 1, 1), (w1_pass, 1, 1),
+        for h in range(HALVES):
+            for tt in range(TOKEN_TILES):
+                w2_pass(h, tt, 0, False)
+        for one_pass, h, a, stop in (
+            (w1_pass, 0, 0, False), (w1_pass, 0, 1, False), (w2_pass, 0, 1, True),
+            (w1_pass, 1, 0, False), (w2_pass, 1, 1, False), (w1_pass, 1, 1, True),
         ):
             for tt in range(TOKEN_TILES):
-                one_pass(h, tt, a)
+                one_pass(h, tt, a, stop)
 
         summed = [keep.tile([P, TOKEN_TILES, HALF], F32, name=f"summed{h}") for h in range(HALVES)]
         result = [keep.tile([P, TOKEN_TILES, HALF], F32, name=f"result{h}") for h in range(HALVES)]
@@ -239,10 +240,7 @@ def tile_list_tabfield_tm_gelu_kernel(
                 summed[h][:, tt, first:last], acc[h][tt][:, first:last],
                 bias_row[:, h * HALF + first : h * HALF + last], mybir.AluOpType.add,
             )
-            nc.scalar.activation(
-                result[h][:, tt, first:last], summed[h][:, tt, first:last],
-                mybir.ActivationFunctionType.Gelu_apprx_tanh,
-            )
+            nc.scalar.activation(result[h][:, tt, first:last], summed[h][:, tt, first:last], GELU)
 
         for h, tt, first, last in ((0, 0, 0, HALF), (0, 1, 0, HALF), (1, 0, 0, HALF), (1, 1, 0, P), (1, 1, P, HALF)):
             finish(h, tt, first, last)

@@ -30,7 +30,6 @@ KIB = 1024
 SPREAD = 4
 PLANE = M + S
 LATER = (FIELDS - 1) * S
-VECTOR_COLS = 152
 
 
 def tile_list_tabfield_tm_gelu_kernel(
@@ -68,7 +67,11 @@ def tile_list_tabfield_tm_gelu_kernel(
             reuse.tile([P, T], I32, name="tab_words1", align_bytes=64, offset=32 * KIB),
         ]
         w0_codes = keep.tile([P, PASSES, 2 * M // 4], I32, name="w0_codes", align_bytes=64)
-        w2_raw0 = keep.tile([P, PACK, M], F32, name="w2_raw0", align_bytes=64)
+        w2_rows = w2.rearrange("(a p u j) n -> a u p j n", a=PASSES, u=2, j=2)
+        early_pairs = [
+            keep.tile([P, 2, M], F32, name="early_pair0", align_bytes=64),
+            reuse.tile([P, 2, M], F32, name="early_pair1", align_bytes=64, offset=0),
+        ]
 
         nc.sync.dma_start(w0_codes[:], w0_words.rearrange("a p c -> p a c").bitcast(I32))
         nc.sync.dma_start(offsets[:], offs)
@@ -81,10 +84,10 @@ def tile_list_tabfield_tm_gelu_kernel(
             nc.sync.dma_start(
                 tab_words[a][:], tab[a, 0 : K_PASS * T].rearrange("(p w) -> p w", p=P).bitcast(I32)
             )
-        nc.sync.dma_start(w2_raw0[:], w2[0:K_PASS, :].rearrange("(p j) n -> p j n", j=PACK))
+        nc.sync.dma_start(early_pairs[0][:], w2_rows[0, 0])
 
         picked_words = [keep.tile([P, FIELDS * S], U32, name=f"picked_words{a}", align_bytes=64) for a in range(PASSES)]
-        first_scales = keep.tile([P, S], U8, name="first_scales", align_bytes=64)
+        first_scales = reuse.tile([P, S], U8, name="first_scales", align_bytes=64, offset=0)
         later_scales = keep.tile([P, LATER], U8, name="later_scales", align_bytes=64)
         w2_codes = keep.tile([P, HALVES, PASSES, HALF], U32, name="w2_codes", align_bytes=64)
         w2_scales = {
@@ -101,12 +104,6 @@ def tile_list_tabfield_tm_gelu_kernel(
         def gather(dst, window, first, last):
             nc.vector.tensor_copy(dst[:], window.indirect(offsets[:, first * S // 16 : last * S // 16]))
 
-        def interleave(copy, h, first, last):
-            copy(
-                w2_bf16[h, 0][:, first:last, :].rearrange("p (c i) j -> p c j i", i=4),
-                w2_raw0[:, :, h * HALF + first : h * HALF + last].rearrange("p j (c i) -> p c j i", i=4),
-            )
-
         def quantize(h, a):
             nc.vector.quantize_mx(
                 out=w2_codes[:, h, a, :].bitcast(FP8X4),
@@ -118,10 +115,11 @@ def tile_list_tabfield_tm_gelu_kernel(
         gather(first_scales, scale_window[:].bitcast(U8), 0, 1)
         nc.vector.tensor_copy(staged[:, M // 4 : PLANE // 4], first_scales[:].bitcast(I32))
         for quad in (0, 2, 1, 3):
-            nc.scalar.dma_start(
+            nc.sync.dma_start(
                 planes[QUAD * quad : QUAD * quad + ROWS, :, :].rearrange("p a n -> p (a n)"),
                 staged[QUAD * quad : QUAD * (quad + 1) : SPREAD, :],
             )
+        nc.sync.dma_start(early_pairs[1][:], w2_rows[0, 1])
         for quad in (0, 2, 1, 3):
             nc.gpsimd.dma_start(
                 later_planes[QUAD * quad + 2 * ROWS : QUAD * quad + 3 * ROWS, :, :].rearrange("p a n -> p (a n)"),
@@ -139,14 +137,17 @@ def tile_list_tabfield_tm_gelu_kernel(
         nc.scalar.copy(bias[:], bias_bank[:].rearrange("j c p -> j p c"))
         bias_row = bias[:].rearrange("j p c -> j (p c)")
 
-        w2_last = w2[K_PASS:K, :].rearrange("(p u j) n -> p u j n", u=2, j=2)
         first_pair = reuse.tile([P, 2, M], F32, name="first_pair", align_bytes=64, offset=12 * KIB + 64)
-        nc.sync.dma_start(first_pair[:], w2_last[:, 0, :, :])
-        w2_pairs = {(0, h): first_pair[:, :, h * HALF : (h + 1) * HALF] for h in range(HALVES)}
+        nc.sync.dma_start(first_pair[:], w2_rows[1, 0])
+        w2_pairs = {
+            (a, u, h): pair[:, :, h * HALF : (h + 1) * HALF]
+            for a, u, pair in ((0, 0, early_pairs[0]), (0, 1, early_pairs[1]), (1, 0, first_pair))
+            for h in range(HALVES)
+        }
         second_pair = reuse.tile([P, 2, M], F32, name="second_pair", align_bytes=64, offset=16 * KIB + 64)
-        nc.sync.dma_start(second_pair[:], w2_last[:, 1, :, :])
+        nc.sync.dma_start(second_pair[:], w2_rows[1, 1])
         for h in range(HALVES):
-            w2_pairs[1, h] = second_pair[:, :, h * HALF : (h + 1) * HALF]
+            w2_pairs[1, 1, h] = second_pair[:, :, h * HALF : (h + 1) * HALF]
         w1_codes = {}
         w1_rows = w1_words.rearrange("a p n i -> p a (n i)").bitcast(I32)
         for h in range(HALVES):
@@ -154,24 +155,26 @@ def tile_list_tabfield_tm_gelu_kernel(
                 start = (20 + PASSES * h + a) * KIB + 64
                 w1_codes[h, a] = reuse.tile([P, HALF], I32, name=f"w1_codes{h}{a}", align_bytes=64, offset=start)
                 nc.sync.dma_start(w1_codes[h, a][:], w1_rows[:, a, h * HALF : (h + 1) * HALF])
-        for h in range(HALVES):
-            interleave(nc.scalar.copy, h, 0, HALF - VECTOR_COLS)
-            interleave(nc.vector.tensor_copy, h, HALF - VECTOR_COLS, HALF)
-        for h in range(HALVES):
-            quantize(h, 0)
 
-        def interleave_pair(copy, u, h, first, last):
+        def interleave_pair(copy, a, u, h, first, last):
             copy(
-                w2_bf16[h, 1][:, first:last, 2 * u : 2 * u + 2].rearrange("p (c i) j -> p c j i", i=4),
-                w2_pairs[u, h][:, :, first:last].rearrange("p j (c i) -> p c j i", i=4),
+                w2_bf16[h, a][:, first:last, 2 * u : 2 * u + 2].rearrange("p (c i) j -> p c j i", i=4),
+                w2_pairs[a, u, h][:, :, first:last].rearrange("p j (c i) -> p c j i", i=4),
             )
 
-        interleave_pair(nc.vector.tensor_copy, 0, 0, 0, 256)
-        interleave_pair(nc.scalar.copy, 0, 1, 0, 192)
-        interleave_pair(nc.vector.tensor_copy, 0, 1, 192, 256)
-        interleave_pair(nc.vector.tensor_copy, 1, 0, 0, 256)
-        interleave_pair(nc.scalar.copy, 1, 1, 0, 144)
-        interleave_pair(nc.vector.tensor_copy, 1, 1, 144, 256)
+        interleave_pair(nc.vector.tensor_copy, 0, 0, 0, 0, 256)
+        interleave_pair(nc.scalar.copy, 0, 0, 1, 0, 256)
+        interleave_pair(nc.vector.tensor_copy, 0, 1, 0, 0, 256)
+        interleave_pair(nc.scalar.copy, 0, 1, 1, 0, 144)
+        interleave_pair(nc.vector.tensor_copy, 0, 1, 1, 144, 256)
+        for h in range(HALVES):
+            quantize(h, 0)
+        interleave_pair(nc.vector.tensor_copy, 1, 0, 0, 0, 256)
+        interleave_pair(nc.scalar.copy, 1, 0, 1, 0, 192)
+        interleave_pair(nc.vector.tensor_copy, 1, 0, 1, 192, 256)
+        interleave_pair(nc.vector.tensor_copy, 1, 1, 0, 0, 256)
+        interleave_pair(nc.scalar.copy, 1, 1, 1, 0, 144)
+        interleave_pair(nc.vector.tensor_copy, 1, 1, 1, 144, 256)
         for h in range(HALVES):
             quantize(h, 1)
 
@@ -204,7 +207,7 @@ def tile_list_tabfield_tm_gelu_kernel(
                     table_pass(
                         h, tt, 0, a, slice(c0, c0 + P),
                         w0_bytes[:, a, 2 * n0 : 2 * (n0 + P)].bitcast(FP4X4),
-                        plane_bytes[:, a, n0 : n0 + P], a == PASSES - 1 and c0 == 0, False,
+                        plane_bytes[:, a, n0 : n0 + P], a == 0 and c0 == 0, False,
                     )
 
         def w1_pass(h, tt, a, stop):
@@ -218,7 +221,7 @@ def tile_list_tabfield_tm_gelu_kernel(
                 h, tt, 2, a, slice(0, HALF), w2_codes[:, h, a, :].bitcast(FP8X4), w2_scales[h, a][:], False, stop,
             )
 
-        for a in reversed(range(PASSES)):
+        for a in range(PASSES):
             for h in range(HALVES):
                 w0_passes(h, a)
         for h in range(HALVES):

@@ -163,18 +163,19 @@ def tile_list_tabfield_tm_gelu_kernel(
             )
 
         interleave_pair(nc.vector.tensor_copy, 0, 0, 0, 0, 256)
-        interleave_pair(nc.scalar.copy, 0, 0, 1, 0, 256)
+        interleave_pair(nc.scalar.copy, 0, 0, 1, 0, 160)
+        interleave_pair(nc.vector.tensor_copy, 0, 0, 1, 160, 256)
         interleave_pair(nc.vector.tensor_copy, 0, 1, 0, 0, 256)
-        interleave_pair(nc.scalar.copy, 0, 1, 1, 0, 144)
-        interleave_pair(nc.vector.tensor_copy, 0, 1, 1, 144, 256)
+        interleave_pair(nc.scalar.copy, 0, 1, 1, 0, 96)
+        interleave_pair(nc.vector.tensor_copy, 0, 1, 1, 96, 256)
         for h in range(HALVES):
             quantize(h, 0)
         interleave_pair(nc.vector.tensor_copy, 1, 0, 0, 0, 256)
-        interleave_pair(nc.scalar.copy, 1, 0, 1, 0, 192)
-        interleave_pair(nc.vector.tensor_copy, 1, 0, 1, 192, 256)
+        interleave_pair(nc.scalar.copy, 1, 0, 1, 0, 128)
+        interleave_pair(nc.vector.tensor_copy, 1, 0, 1, 128, 256)
         interleave_pair(nc.vector.tensor_copy, 1, 1, 0, 0, 256)
-        interleave_pair(nc.scalar.copy, 1, 1, 1, 0, 144)
-        interleave_pair(nc.vector.tensor_copy, 1, 1, 1, 144, 256)
+        interleave_pair(nc.scalar.copy, 1, 1, 1, 0, 128)
+        interleave_pair(nc.vector.tensor_copy, 1, 1, 1, 128, 256)
         for h in range(HALVES):
             quantize(h, 1)
 
@@ -227,12 +228,16 @@ def tile_list_tabfield_tm_gelu_kernel(
         for h in range(HALVES):
             for tt in range(TOKEN_TILES):
                 w2_pass(h, tt, 0, False)
-        for one_pass, h, a, stop in (
-            (w1_pass, 0, 0, False), (w1_pass, 0, 1, False), (w2_pass, 0, 1, True),
-            (w1_pass, 1, 0, False), (w2_pass, 1, 1, False), (w1_pass, 1, 1, True),
-        ):
+        for a in range(PASSES):
             for tt in range(TOKEN_TILES):
-                one_pass(h, tt, a, stop)
+                w1_pass(0, tt, a, False)
+        for tt in range(TOKEN_TILES):
+            w2_pass(0, tt, 1, True)
+        for tt in range(TOKEN_TILES):
+            w1_pass(1, tt, 0, False)
+        for tt in range(TOKEN_TILES):
+            w1_pass(1, tt, 1, False)
+            w2_pass(1, tt, 1, True)
 
         summed = [keep.tile([P, TOKEN_TILES, HALF], F32, name=f"summed{h}") for h in range(HALVES)]
         result = [keep.tile([P, TOKEN_TILES, HALF], F32, name=f"result{h}") for h in range(HALVES)]

@@ -48,9 +48,6 @@ def tile_list_tabfield_tm_gelu_kernel(
         nc.gpsimd.memset(scale_window[:, T // 8 : T // 4], 0)
         w1_planes = keep.tile([P, PASSES, M // 4], I32, name="w1_planes", align_bytes=64)
         nc.vector.memset(w1_planes[:], 0)
-        warm = keep.tile([P, 2], F32, name="warm")
-        nc.vector.memset(warm[:, 0:1], 0.0)
-        nc.scalar.activation(warm[:, 1:2], warm[:, 0:1], GELU)
         nc.vector.memset(planes[:], 0)
         later_planes = keep.tile([P, PASSES, LATER // 4], I32, name="later_planes", align_bytes=64)
         nc.vector.memset(later_planes[:], 0)

@@ -44,17 +44,15 @@ def tile_list_tabfield_tm_gelu_kernel(
         scale_window = keep.tile([P, T // 4], I32, name="scale_window", align_bytes=64)
         staged = keep.tile([P, PLANE // 4], I32, name="staged", align_bytes=64)
         planes = keep.tile([P, PASSES, PLANE // 4], I32, name="planes", align_bytes=64)
-        nc.vector.memset(scale_window[:, 0 : T // 8], 0)
-        nc.gpsimd.memset(scale_window[:, T // 8 : T // 4], 0)
-        w1_planes = keep.tile([P, PASSES, M // 4], I32, name="w1_planes", align_bytes=64)
-        nc.vector.memset(w1_planes[:], 0)
+        nc.vector.memset(scale_window[:], 0)
+        weight_planes = keep.tile([P, M], U8, name="weight_planes", align_bytes=64)
         nc.vector.memset(planes[:], 0)
         later_planes = keep.tile([P, PASSES, LATER // 4], I32, name="later_planes", align_bytes=64)
         nc.vector.memset(later_planes[:], 0)
         for quad in range(P // QUAD):
             nc.gpsimd.dma_start(
-                w1_planes[QUAD * quad + ROWS : QUAD * quad + 2 * ROWS, :, :],
-                w1_scales[:, ROWS * quad : ROWS * (quad + 1), :].rearrange("a r n -> r a n").bitcast(I32),
+                weight_planes[QUAD * quad + ROWS : QUAD * quad + (1 + PASSES) * ROWS, :].bitcast(I32),
+                w1_scales[:, ROWS * quad : ROWS * (quad + 1), :].bitcast(I32),
             )
 
         offsets = keep.tile([P, FIELDS * S // 16], U16, name="offsets")
@@ -87,10 +85,11 @@ def tile_list_tabfield_tm_gelu_kernel(
         first_scales = reuse.tile([P, S], U8, name="first_scales", align_bytes=64, offset=0)
         later_scales = keep.tile([P, LATER], U8, name="later_scales", align_bytes=64)
         w2_codes = keep.tile([P, HALVES, PASSES, HALF], U32, name="w2_codes", align_bytes=64)
+        last_planes = keep.tile([P, M], U8, name="last_planes", align_bytes=64)
         w2_scales = {
-            (h, a): keep.tile([P, HALF], U8, name=f"w2_scales_{h}{a}", align_bytes=64)
+            (h, a): tile[:, h * HALF : (h + 1) * HALF]
             for h in range(HALVES)
-            for a in range(PASSES)
+            for a, tile in enumerate((weight_planes, last_planes))
         }
         w2_bf16 = {
             (h, a): keep.tile([P, HALF, PACK], BF16, name=f"w2_bf16_{h}{a}", align_bytes=64)
@@ -104,7 +103,7 @@ def tile_list_tabfield_tm_gelu_kernel(
         def quantize(h, a):
             nc.vector.quantize_mx(
                 out=w2_codes[:, h, a, :].bitcast(FP8X4),
-                scales=w2_scales[h, a][:],
+                scales=w2_scales[h, a],
                 in_=w2_bf16[h, a][:].rearrange("p n j -> p (n j)"),
             )
 
@@ -177,7 +176,6 @@ def tile_list_tabfield_tm_gelu_kernel(
             quantize(h, 1)
 
         plane_bytes = planes[:].bitcast(U8)
-        w1_scale_bytes = w1_planes[ROWS:P, :, :].bitcast(U8)
         later_bytes = later_planes[2 * ROWS : P, :, :].bitcast(U8)
         w0_bytes = w0_codes[:].bitcast(U8)
         acc = [
@@ -211,12 +209,12 @@ def tile_list_tabfield_tm_gelu_kernel(
         def w1_pass(h, tt, a, stop):
             table_pass(
                 h, tt, 1, a, slice(0, HALF), w1_codes[h, a][:].bitcast(FP8X4),
-                w1_scale_bytes[:, a, h * HALF : (h + 1) * HALF], False, stop,
+                weight_planes[ROWS * (1 + a) : P, h * HALF : (h + 1) * HALF], False, stop,
             )
 
         def w2_pass(h, tt, a, stop):
             table_pass(
-                h, tt, 2, a, slice(0, HALF), w2_codes[:, h, a, :].bitcast(FP8X4), w2_scales[h, a][:], False, stop,
+                h, tt, 2, a, slice(0, HALF), w2_codes[:, h, a, :].bitcast(FP8X4), w2_scales[h, a], False, stop,
             )
 
         for a in range(PASSES):

@@ -1,7 +1,6 @@
 from contextlib import ExitStack
 
 import concourse.mybir as mybir
-from concourse.masks import make_identity
 
 K, M, T, S = 1024, 512, 2048, 256
 FIELDS = 3
@@ -44,11 +43,21 @@ def tile_list_tabfield_tm_gelu_kernel(
         scale_window = keep.tile([P, T // 4], I32, name="scale_window", align_bytes=64)
         staged = keep.tile([P, PLANE // 4], I32, name="staged", align_bytes=64)
         planes = keep.tile([P, PASSES, PLANE // 4], I32, name="planes", align_bytes=64)
-        nc.vector.memset(scale_window[:], 0)
+        ramp = keep.tile([P, P], F32, name="ramp")
+        nc.gpsimd.iota(ramp[:], [[1, P]], base=0, channel_multiplier=-1, allow_small_or_imprecise_dtypes=True)
+
+        def zero(words):
+            count = words.shape[1]
+            nc.vector.memset(words[:, 0 : count - 1], 0)
+            nc.vector.memset(words[:, count - 1 : count], 0)
+
+        zero(scale_window[:])
+        identity = keep.tile([P, P], F32, name="identity")
+        nc.vector.tensor_scalar(identity[:], ramp[:], 0.0, None, mybir.AluOpType.is_equal)
         weight_planes = keep.tile([P, M], U8, name="weight_planes", align_bytes=64)
-        nc.vector.memset(planes[:], 0)
+        zero(planes[:].rearrange("p a n -> p (a n)"))
         later_planes = keep.tile([P, PASSES, LATER // 4], I32, name="later_planes", align_bytes=64)
-        nc.vector.memset(later_planes[:], 0)
+        zero(later_planes[:].rearrange("p a n -> p (a n)"))
         for quad in range(P // QUAD):
             nc.gpsimd.dma_start(
                 weight_planes[QUAD * quad + ROWS : QUAD * quad + (1 + PASSES) * ROWS, :].bitcast(I32),
@@ -124,8 +133,6 @@ def tile_list_tabfield_tm_gelu_kernel(
         for a in range(PASSES):
             gather(picked_words[a], tab_words[a][:].bitcast(U32), 0, FIELDS)
 
-        identity = keep.tile([P, P], F32, name="identity")
-        make_identity(nc, identity[:])
         bias_bank = psum.tile([P, PACK, P], F32, name="bias_bank")
         for c in range(PACK):
             nc.tensor.transpose(bias_bank[:, c, :], b_cols[:, c : c + 1].to_broadcast([P, P]), identity[:])

@@ -25,10 +25,22 @@ HALVES = 2
 TOKEN_TILES = S // P
 QUAD = 32
 ROWS = 4
+WORD = 4
+LIST_ROWS = 16
 KIB = 1024
+LINE = 256
 SPREAD = 4
 PLANE = M + S
 LATER = (FIELDS - 1) * S
+MOVE_ORDER = (0, 2, 1, 3)
+SCALAR_COLUMNS = ((384, 192), (256, 96))
+FIRST_SHARE = 96
+SEAM = 8
+
+FIELD0_SCALES_AT = 0
+TABLE_AT = (16 * KIB, 32 * KIB)
+OVERLAP = LINE
+LATE_AT = TABLE_AT[0] - 4 * KIB + OVERLAP
 
 
 def tile_list_tabfield_tm_gelu_kernel(
@@ -40,9 +52,9 @@ def tile_list_tabfield_tm_gelu_kernel(
         reuse = ctx.enter_context(tc.tile_pool(name="reuse", bufs=1))
         psum = ctx.enter_context(tc.psum_pool(name="psum", bufs=1))
 
-        scale_window = keep.tile([P, T // 4], I32, name="scale_window", align_bytes=64)
-        staged = keep.tile([P, PLANE // 4], I32, name="staged", align_bytes=64)
-        planes = keep.tile([P, PASSES, PLANE // 4], I32, name="planes", align_bytes=64)
+        scale_window = keep.tile([P, T // WORD], I32, name="scale_window", align_bytes=LINE)
+        staged = keep.tile([P, PLANE // WORD], I32, name="staged", align_bytes=LINE)
+        first_planes = keep.tile([P, PASSES, PLANE // WORD], I32, name="first_planes", align_bytes=LINE)
         ramp = keep.tile([P, P], F32, name="ramp")
         nc.gpsimd.iota(ramp[:], [[1, P]], base=0, channel_multiplier=-1, allow_small_or_imprecise_dtypes=True)
 
@@ -54,9 +66,9 @@ def tile_list_tabfield_tm_gelu_kernel(
         zero(scale_window[:])
         identity = keep.tile([P, P], F32, name="identity")
         nc.vector.tensor_scalar(identity[:], ramp[:], 0.0, None, mybir.AluOpType.is_equal)
-        weight_planes = keep.tile([P, M], U8, name="weight_planes", align_bytes=64)
-        zero(planes[:].rearrange("p a n -> p (a n)"))
-        later_planes = keep.tile([P, PASSES, LATER // 4], I32, name="later_planes", align_bytes=64)
+        weight_planes = keep.tile([P, M], U8, name="weight_planes", align_bytes=LINE)
+        zero(first_planes[:].rearrange("p a n -> p (a n)"))
+        later_planes = keep.tile([P, PASSES, LATER // WORD], I32, name="later_planes", align_bytes=LINE)
         zero(later_planes[:].rearrange("p a n -> p (a n)"))
         for quad in range(P // QUAD):
             nc.gpsimd.dma_start(
@@ -64,22 +76,21 @@ def tile_list_tabfield_tm_gelu_kernel(
                 w1_scales[:, ROWS * quad : ROWS * (quad + 1), :].bitcast(I32),
             )
 
-        offsets = keep.tile([P, FIELDS * S // 16], U16, name="offsets")
-        b_cols = keep.tile([P, PACK], F32, name="b_cols")
+        offsets = keep.tile([P, FIELDS * S // LIST_ROWS], U16, name="offsets", align_bytes=LINE)
+        b_cols = keep.tile([P, PACK], F32, name="b_cols", align_bytes=LINE)
         tab_words = [
-            reuse.tile([P, T], I32, name="tab_words0", align_bytes=64, offset=16 * KIB),
-            reuse.tile([P, T], I32, name="tab_words1", align_bytes=64, offset=32 * KIB),
+            reuse.tile([P, T], I32, name=f"tab_words{a}", align_bytes=LINE, offset=TABLE_AT[a]) for a in range(PASSES)
         ]
-        w0_codes = keep.tile([P, PASSES, 2 * M // 4], I32, name="w0_codes", align_bytes=64)
+        w0_codes = keep.tile([P, PASSES, 2 * M // WORD], I32, name="w0_codes", align_bytes=LINE)
         w2_rows = w2.rearrange("(a p u j) n -> a u p j n", a=PASSES, u=2, j=2)
-        early_pairs = [
-            keep.tile([P, 2, M], F32, name="early_pair0", align_bytes=64),
-            reuse.tile([P, 2, M], F32, name="early_pair1", align_bytes=64, offset=0),
-        ]
+        w2_pairs = {
+            (0, 0): keep.tile([P, 2, M], F32, name="w2_pair00", align_bytes=LINE),
+            (0, 1): reuse.tile([P, 2, M], F32, name="w2_pair01", align_bytes=LINE, offset=FIELD0_SCALES_AT),
+        }
 
         nc.sync.dma_start(w0_codes[:], w0_words.rearrange("a p c -> p a c").bitcast(I32))
         nc.sync.dma_start(offsets[:], offs)
-        nc.sync.dma_start(staged[0:P:SPREAD, 0 : M // 4], w0_scales.rearrange("a q n -> q a n").bitcast(I32))
+        nc.sync.dma_start(staged[0:P:SPREAD, 0 : M // WORD], w0_scales.rearrange("a q n -> q a n").bitcast(I32))
         nc.sync.dma_start(b_cols[:], b.rearrange("(p c) -> p c", c=PACK))
         nc.sync.dma_start(
             scale_window[0:P:SPREAD, :], tab[:, K_PASS * T :].rearrange("a (q t) -> q a t", t=T).bitcast(I32)
@@ -88,44 +99,37 @@ def tile_list_tabfield_tm_gelu_kernel(
             nc.sync.dma_start(
                 tab_words[a][:], tab[a, 0 : K_PASS * T].rearrange("(p w) -> p w", p=P).bitcast(I32)
             )
-        nc.sync.dma_start(early_pairs[0][:], w2_rows[0, 0])
+        nc.sync.dma_start(w2_pairs[0, 0][:], w2_rows[0, 0])
 
-        picked_words = [keep.tile([P, FIELDS * S], U32, name=f"picked_words{a}", align_bytes=64) for a in range(PASSES)]
-        first_scales = reuse.tile([P, S], U8, name="first_scales", align_bytes=64, offset=0)
-        later_scales = keep.tile([P, LATER], U8, name="later_scales", align_bytes=64)
-        w2_codes = keep.tile([P, HALVES, PASSES, HALF], U32, name="w2_codes", align_bytes=64)
-        last_planes = keep.tile([P, M], U8, name="last_planes", align_bytes=64)
+        warm_up = keep.tile([P, 1], F32, name="warm_up")
+        nc.scalar.activation(warm_up[:], b_cols[:, 0:1], GELU)
+
+        picked_words = [keep.tile([P, FIELDS * S], U32, name=f"picked_words{a}", align_bytes=LINE) for a in range(PASSES)]
+        first_scales = reuse.tile([P, S], U8, name="first_scales", align_bytes=LINE, offset=FIELD0_SCALES_AT)
+        later_scales = keep.tile([P, LATER], U8, name="later_scales", align_bytes=LINE)
+        w2_codes = keep.tile([P, HALVES, PASSES, HALF], U32, name="w2_codes", align_bytes=LINE)
+        w2_last_plane = keep.tile([P, M], U8, name="w2_last_plane", align_bytes=LINE)
         w2_scales = {
             (h, a): tile[:, h * HALF : (h + 1) * HALF]
             for h in range(HALVES)
-            for a, tile in enumerate((weight_planes, last_planes))
+            for a, tile in enumerate((weight_planes, w2_last_plane))
         }
-        w2_bf16 = {
-            (h, a): keep.tile([P, HALF, PACK], BF16, name=f"w2_bf16_{h}{a}", align_bytes=64)
-            for h in range(HALVES)
-            for a in range(PASSES)
-        }
+        w2_bf16 = [keep.tile([P, M, PACK], BF16, name=f"w2_bf16_{a}", align_bytes=LINE) for a in range(PASSES)]
 
-        def gather(dst, window, first, last):
-            nc.vector.tensor_copy(dst[:], window.indirect(offsets[:, first * S // 16 : last * S // 16]))
-
-        def quantize(h, a):
-            nc.vector.quantize_mx(
-                out=w2_codes[:, h, a, :].bitcast(FP8X4),
-                scales=w2_scales[h, a],
-                in_=w2_bf16[h, a][:].rearrange("p n j -> p (n j)"),
-            )
+        def gather(dst, window, first_field, end_field):
+            columns = slice(first_field * S // LIST_ROWS, end_field * S // LIST_ROWS)
+            nc.vector.tensor_copy(dst[:], window.indirect(offsets[:, columns]))
 
         gather(later_scales, scale_window[:].bitcast(U8), 1, FIELDS)
         gather(first_scales, scale_window[:].bitcast(U8), 0, 1)
-        nc.vector.tensor_copy(staged[:, M // 4 : PLANE // 4], first_scales[:].bitcast(I32))
-        for quad in (0, 2, 1, 3):
+        nc.vector.tensor_copy(staged[:, M // WORD : PLANE // WORD], first_scales[:].bitcast(I32))
+        for quad in MOVE_ORDER:
             nc.sync.dma_start(
-                planes[QUAD * quad : QUAD * quad + ROWS, :, :].rearrange("p a n -> p (a n)"),
+                first_planes[QUAD * quad : QUAD * quad + ROWS, :, :].rearrange("p a n -> p (a n)"),
                 staged[QUAD * quad : QUAD * (quad + 1) : SPREAD, :],
             )
-        nc.sync.dma_start(early_pairs[1][:], w2_rows[0, 1])
-        for quad in (0, 2, 1, 3):
+        nc.sync.dma_start(w2_pairs[0, 1][:], w2_rows[0, 1])
+        for quad in MOVE_ORDER:
             nc.gpsimd.dma_start(
                 later_planes[QUAD * quad + 2 * ROWS : QUAD * quad + 3 * ROWS, :, :].rearrange("p a n -> p (a n)"),
                 later_scales[QUAD * quad : QUAD * (quad + 1) : SPREAD, :].bitcast(I32),
@@ -140,118 +144,124 @@ def tile_list_tabfield_tm_gelu_kernel(
         nc.scalar.copy(bias[:], bias_bank[:].rearrange("j c p -> j p c"))
         bias_row = bias[:].rearrange("j p c -> j (p c)")
 
-        first_pair = reuse.tile([P, 2, M], F32, name="first_pair", align_bytes=64, offset=12 * KIB + 64)
-        nc.sync.dma_start(first_pair[:], w2_rows[1, 0])
-        w2_pairs = {
-            (a, u, h): pair[:, :, h * HALF : (h + 1) * HALF]
-            for a, u, pair in ((0, 0, early_pairs[0]), (0, 1, early_pairs[1]), (1, 0, first_pair))
-            for h in range(HALVES)
-        }
-        second_pair = reuse.tile([P, 2, M], F32, name="second_pair", align_bytes=64, offset=16 * KIB + 64)
-        nc.sync.dma_start(second_pair[:], w2_rows[1, 1])
-        for h in range(HALVES):
-            w2_pairs[1, 1, h] = second_pair[:, :, h * HALF : (h + 1) * HALF]
+        w2_pairs[1, 0] = reuse.tile([P, 2, M], F32, name="w2_pair10", align_bytes=LINE, offset=LATE_AT)
+        nc.sync.dma_start(w2_pairs[1, 0][:], w2_rows[1, 0])
+        last_run = reuse.tile([P, 2 * M], F32, name="last_run", align_bytes=LINE, offset=LATE_AT + 4 * KIB)
+        last_rows = w2_rows[1, 1].rearrange("p j n -> p (j n)")
+        for first, last in ((0, M + HALF), (M + HALF, 2 * M)):
+            nc.sync.dma_start(last_run[:, first:last], last_rows[:, first:last])
+        w2_pairs[1, 1] = last_run[:].rearrange("p (j n) -> p j n", j=2)
         w1_codes = {}
         w1_rows = w1_words.rearrange("a p n i -> p a (n i)").bitcast(I32)
-        for h in range(HALVES):
-            for a in range(PASSES):
-                start = (20 + PASSES * h + a) * KIB + 64
-                w1_codes[h, a] = reuse.tile([P, HALF], I32, name=f"w1_codes{h}{a}", align_bytes=64, offset=start)
-                nc.sync.dma_start(w1_codes[h, a][:], w1_rows[:, a, h * HALF : (h + 1) * HALF])
+        for a in range(PASSES):
+            start = LATE_AT + (8 + a) * KIB
+            w1_codes[0, a] = reuse.tile([P, HALF], I32, name=f"w1_first{a}", align_bytes=LINE, offset=start)[:]
+            nc.sync.dma_start(w1_codes[0, a], w1_rows[:, a, 0:HALF])
+        w1_second = reuse.tile([P, PASSES, HALF], I32, name="w1_second", align_bytes=LINE, offset=LATE_AT + 10 * KIB)
+        nc.sync.dma_start(w1_second[:], w1_rows[:, :, HALF:M])
+        for a in range(PASSES):
+            w1_codes[1, a] = w1_second[:, a, :]
 
-        def interleave_pair(copy, a, u, h, first, last):
+        def round_columns(copy, a, u, first, last):
             copy(
-                w2_bf16[h, a][:, first:last, 2 * u : 2 * u + 2].rearrange("p (c i) j -> p c j i", i=4),
-                w2_pairs[a, u, h][:, :, first:last].rearrange("p j (c i) -> p c j i", i=4),
+                w2_bf16[a][:, first:last, 2 * u : 2 * u + 2].rearrange("p (c i) j -> p c j i", i=4),
+                w2_pairs[a, u][:, :, first:last].rearrange("p j (c i) -> p c j i", i=4),
             )
 
-        interleave_pair(nc.vector.tensor_copy, 0, 0, 0, 0, 256)
-        interleave_pair(nc.scalar.copy, 0, 0, 1, 0, 160)
-        interleave_pair(nc.vector.tensor_copy, 0, 0, 1, 160, 256)
-        interleave_pair(nc.vector.tensor_copy, 0, 1, 0, 0, 256)
-        interleave_pair(nc.scalar.copy, 0, 1, 1, 0, 96)
-        interleave_pair(nc.vector.tensor_copy, 0, 1, 1, 96, 256)
-        for h in range(HALVES):
-            quantize(h, 0)
-        interleave_pair(nc.vector.tensor_copy, 1, 0, 0, 0, 256)
-        interleave_pair(nc.scalar.copy, 1, 0, 1, 0, 128)
-        interleave_pair(nc.vector.tensor_copy, 1, 0, 1, 128, 256)
-        interleave_pair(nc.vector.tensor_copy, 1, 1, 0, 0, 256)
-        interleave_pair(nc.scalar.copy, 1, 1, 1, 0, 128)
-        interleave_pair(nc.vector.tensor_copy, 1, 1, 1, 128, 256)
-        for h in range(HALVES):
-            quantize(h, 1)
+        def quantize_halves(a):
+            for h in range(HALVES):
+                nc.vector.quantize_mx(
+                    out=w2_codes[:, h, a, :].bitcast(FP8X4),
+                    scales=w2_scales[h, a],
+                    in_=w2_bf16[a][:, h * HALF : (h + 1) * HALF, :].rearrange("p n j -> p (n j)"),
+                )
 
-        plane_bytes = planes[:].bitcast(U8)
+        def round_pair(a, u):
+            split = M - SCALAR_COLUMNS[a][u]
+            round_columns(nc.vector.tensor_copy, a, u, 0, min(split, HALF))
+            round_columns(nc.scalar.copy, a, u, split, M)
+            if split > HALF:
+                round_columns(nc.vector.tensor_copy, a, u, HALF, split)
+
+        round_pair(0, 0)
+        round_pair(0, 1)
+        quantize_halves(0)
+        round_pair(1, 0)
+        round_columns(nc.scalar.copy, 1, 1, 0, FIRST_SHARE)
+        round_columns(nc.vector.tensor_copy, 1, 1, FIRST_SHARE, HALF - SEAM)
+        round_columns(nc.scalar.copy, 1, 1, M - SCALAR_COLUMNS[1][1], M)
+        round_columns(nc.vector.tensor_copy, 1, 1, HALF - SEAM, HALF + SEAM)
+        round_columns(nc.vector.tensor_copy, 1, 1, HALF + SEAM, M - SCALAR_COLUMNS[1][1])
+        quantize_halves(1)
+
+        first_bytes = first_planes[:].bitcast(U8)
         later_bytes = later_planes[2 * ROWS : P, :, :].bitcast(U8)
         w0_bytes = w0_codes[:].bitcast(U8)
-        acc = [
-            [psum.tile([P, HALF], F32, name=f"acc{h}{tt}") for tt in range(TOKEN_TILES)] for h in range(HALVES)
+        half_sums = [
+            [(0, 0, HALF), (1, 0, HALF)],
+            [(0, HALF, HALF), (1, HALF, P), (1, HALF + P, P)],
         ]
+        sums = half_sums[0] + half_sums[1]
+        acc = {s: psum.tile([P, s[2]], F32, name=f"acc{s[0]}_{s[1]}") for s in sums}
 
-        def table_pass(h, tt, f, a, cols, rhs, rhs_scale, start, stop):
-            first = f * S + tt * P
+        def table_pass(s, f, a, cols, rhs, rhs_scale, start, stop):
+            token = f * S + s[0] * P
+            if f == 0:
+                token_scales = first_bytes[:, a, M + token : M + token + P]
+            else:
+                token_scales = later_bytes[:, a, token - S : token - S + P]
             nc.tensor.matmul_mx(
-                out=acc[h][tt][:, cols],
-                lhsT=picked_words[a][:, first : first + P].bitcast(FP8X4),
-                lhsT_scale=(
-                    plane_bytes[:, a, M + first : M + first + P] if f == 0 else later_bytes[:, a, first - S : first - S + P]
-                ),
+                out=acc[s][:, cols],
+                lhsT=picked_words[a][:, token : token + P].bitcast(FP8X4),
+                lhsT_scale=token_scales,
                 rhs=rhs,
                 rhs_scale=rhs_scale,
                 start=start,
                 stop=stop,
             )
 
-        def w0_passes(h, a):
-            for tt in range(TOKEN_TILES):
-                for c0 in range(0, HALF, P):
-                    n0 = h * HALF + c0
-                    table_pass(
-                        h, tt, 0, a, slice(c0, c0 + P),
-                        w0_bytes[:, a, 2 * n0 : 2 * (n0 + P)].bitcast(FP4X4),
-                        plane_bytes[:, a, n0 : n0 + P], a == 0 and c0 == 0, False,
-                    )
+        def w0_passes(s, a):
+            for c0 in range(0, s[2], P):
+                n0 = s[1] + c0
+                table_pass(
+                    s, 0, a, slice(c0, c0 + P), w0_bytes[:, a, 2 * n0 : 2 * (n0 + P)].bitcast(FP4X4),
+                    first_bytes[:, a, n0 : n0 + P], a == 0 and c0 == 0, False,
+                )
 
-        def w1_pass(h, tt, a, stop):
+        def w1_pass(s, a):
+            h, c0 = divmod(s[1], HALF)
             table_pass(
-                h, tt, 1, a, slice(0, HALF), w1_codes[h, a][:].bitcast(FP8X4),
-                weight_planes[ROWS * (1 + a) : P, h * HALF : (h + 1) * HALF], False, stop,
+                s, 1, a, slice(0, s[2]), w1_codes[h, a][:, c0 : c0 + s[2]].bitcast(FP8X4),
+                weight_planes[ROWS * (1 + a) : P, s[1] : s[1] + s[2]], False, False,
             )
 
-        def w2_pass(h, tt, a, stop):
+        def w2_pass(s, a):
+            h, c0 = divmod(s[1], HALF)
             table_pass(
-                h, tt, 2, a, slice(0, HALF), w2_codes[:, h, a, :].bitcast(FP8X4), w2_scales[h, a], False, stop,
+                s, 2, a, slice(0, s[2]), w2_codes[:, h, a, c0 : c0 + s[2]].bitcast(FP8X4),
+                w2_scales[h, a][:, c0 : c0 + s[2]], False, a == PASSES - 1,
             )
 
         for a in range(PASSES):
-            for h in range(HALVES):
-                w0_passes(h, a)
-        for h in range(HALVES):
-            for tt in range(TOKEN_TILES):
-                w2_pass(h, tt, 0, False)
+            for s in sums:
+                w0_passes(s, a)
+        for s in sums:
+            w2_pass(s, 0)
         for a in range(PASSES):
-            for tt in range(TOKEN_TILES):
-                w1_pass(0, tt, a, False)
-        for tt in range(TOKEN_TILES):
-            w2_pass(0, tt, 1, True)
-        for tt in range(TOKEN_TILES):
-            w1_pass(1, tt, 0, False)
-        for tt in range(TOKEN_TILES):
-            w1_pass(1, tt, 1, False)
-            w2_pass(1, tt, 1, True)
+            for s in half_sums[0]:
+                w1_pass(s, a)
+        for s in half_sums[0]:
+            w2_pass(s, 1)
+        for s in half_sums[1]:
+            w1_pass(s, 0)
+            w1_pass(s, 1)
+            w2_pass(s, 1)
 
-        summed = [keep.tile([P, TOKEN_TILES, HALF], F32, name=f"summed{h}") for h in range(HALVES)]
-        result = [keep.tile([P, TOKEN_TILES, HALF], F32, name=f"result{h}") for h in range(HALVES)]
         out_view = out.rearrange("(tt p) n -> p tt n", p=P)
-
-        def finish(h, tt, first, last):
-            nc.vector.tensor_tensor(
-                summed[h][:, tt, first:last], acc[h][tt][:, first:last],
-                bias_row[:, h * HALF + first : h * HALF + last], mybir.AluOpType.add,
-            )
-            nc.scalar.activation(result[h][:, tt, first:last], summed[h][:, tt, first:last], GELU)
-
-        for h, tt, first, last in ((0, 0, 0, HALF), (0, 1, 0, HALF), (1, 0, 0, HALF), (1, 1, 0, P), (1, 1, P, HALF)):
-            finish(h, tt, first, last)
-            nc.sync.dma_start(out_view[:, tt, h * HALF + first : h * HALF + last], result[h][:, tt, first:last])
+        for s in sums:
+            tt, first, width = s
+            summed = keep.tile([P, width], F32, name=f"summed{tt}_{first}")
+            result = keep.tile([P, width], F32, name=f"result{tt}_{first}", align_bytes=LINE)
+            nc.vector.tensor_tensor(summed[:], acc[s][:], bias_row[:, first : first + width], mybir.AluOpType.add)
+            nc.scalar.activation(result[:], summed[:], GELU)
+            nc.sync.dma_start(out_view[:, tt, first : first + width], result[:])

@@ -258,10 +258,18 @@ def tile_list_tabfield_tm_gelu_kernel(
             w2_pass(s, 1)
 
         out_view = out.rearrange("(tt p) n -> p tt n", p=P)
+        summed = [keep.tile([P, M], F32, name=f"summed{tt}") for tt in range(TOKEN_TILES)]
+        result = [keep.tile([P, M], F32, name=f"result{tt}", align_bytes=LINE) for tt in range(TOKEN_TILES)]
         for s in sums:
             tt, first, width = s
-            summed = keep.tile([P, width], F32, name=f"summed{tt}_{first}")
-            result = keep.tile([P, width], F32, name=f"result{tt}_{first}", align_bytes=LINE)
-            nc.vector.tensor_tensor(summed[:], acc[s][:], bias_row[:, first : first + width], mybir.AluOpType.add)
-            nc.scalar.activation(result[:], summed[:], GELU)
-            nc.sync.dma_start(out_view[:, tt, first : first + width], result[:])
+            for n0 in range(first, first + width, P):
+                cols = slice(n0, n0 + P)
+                nc.vector.tensor_tensor(
+                    summed[tt][:, cols], acc[s][:, n0 - first : n0 - first + P], bias_row[:, cols], mybir.AluOpType.add
+                )
+                nc.scalar.activation(result[tt][:, cols], summed[tt][:, cols], GELU)
+                if s == sums[0]:
+                    nc.sync.dma_start(out_view[:, tt, cols], result[tt][:, cols])
+                elif (n0 + P) % HALF == 0:
+                    half = slice(n0 + P - HALF, n0 + P)
+                    nc.sync.dma_start(out_view[:, tt, half], result[tt][:, half])

from contextlib import ExitStack

import concourse.mybir as mybir

K, M, T, S = 1024, 512, 2048, 256
FIELDS = 3
FLOPS = 2 * FIELDS * K * M * S

F32 = mybir.dt.float32
BF16 = mybir.dt.bfloat16
I32 = mybir.dt.int32
U32 = mybir.dt.uint32
U16 = mybir.dt.uint16
U8 = mybir.dt.uint8
FP8X4 = mybir.dt.float8_e4m3fn_x4
FP4X4 = mybir.dt.float4_e2m1fn_x4
GELU = mybir.ActivationFunctionType.Gelu_apprx_tanh

P = 128
PACK = 4
K_PASS = P * PACK
PASSES = K // K_PASS
HALF = M // 2
HALVES = 2
TOKEN_TILES = S // P
QUAD = 32
ROWS = 4
WORD = 4
LIST_ROWS = 16
KIB = 1024
LINE = 256
SPREAD = 4
PLANE = M + S
LATER = (FIELDS - 1) * S
MOVE_ORDER = (0, 2, 1, 3)
SCALAR_COLUMNS = ((384, 192), (256, 96))
FIRST_SHARE = 96
SEAM = 8

FIELD0_SCALES_AT = 0
TABLE_AT = (16 * KIB, 32 * KIB)
OVERLAP = LINE
LATE_AT = TABLE_AT[0] - 4 * KIB + OVERLAP


def tile_list_tabfield_tm_gelu_kernel(
    tc, tab, w0_words, w0_scales, w1_words, w1_scales, w2, b, offs, out
):
    nc = tc.nc
    with ExitStack() as ctx:
        keep = ctx.enter_context(tc.tile_pool(name="keep", bufs=1))
        reuse = ctx.enter_context(tc.tile_pool(name="reuse", bufs=1))
        psum = ctx.enter_context(tc.psum_pool(name="psum", bufs=1))

        scale_window = keep.tile([P, T // WORD], I32, name="scale_window", align_bytes=LINE)
        staged = keep.tile([P, PLANE // WORD], I32, name="staged", align_bytes=LINE)
        first_planes = keep.tile([P, PASSES, PLANE // WORD], I32, name="first_planes", align_bytes=LINE)
        ramp = keep.tile([P, P], F32, name="ramp")
        nc.gpsimd.iota(ramp[:], [[1, P]], base=0, channel_multiplier=-1, allow_small_or_imprecise_dtypes=True)

        def zero(words):
            count = words.shape[1]
            nc.vector.memset(words[:, 0 : count - 1], 0)
            nc.vector.memset(words[:, count - 1 : count], 0)

        zero(scale_window[:])
        identity = keep.tile([P, P], F32, name="identity")
        nc.vector.tensor_scalar(identity[:], ramp[:], 0.0, None, mybir.AluOpType.is_equal)
        weight_planes = keep.tile([P, M], U8, name="weight_planes", align_bytes=LINE)
        zero(first_planes[:].rearrange("p a n -> p (a n)"))
        later_planes = keep.tile([P, PASSES, LATER // WORD], I32, name="later_planes", align_bytes=LINE)
        zero(later_planes[:].rearrange("p a n -> p (a n)"))
        for quad in range(P // QUAD):
            nc.gpsimd.dma_start(
                weight_planes[QUAD * quad + ROWS : QUAD * quad + (1 + PASSES) * ROWS, :].bitcast(I32),
                w1_scales[:, ROWS * quad : ROWS * (quad + 1), :].bitcast(I32),
            )

        offsets = keep.tile([P, FIELDS * S // LIST_ROWS], U16, name="offsets", align_bytes=LINE)
        b_cols = keep.tile([P, PACK], F32, name="b_cols", align_bytes=LINE)
        tab_words = [
            reuse.tile([P, T], I32, name=f"tab_words{a}", align_bytes=LINE, offset=TABLE_AT[a]) for a in range(PASSES)
        ]
        w0_codes = keep.tile([P, PASSES, 2 * M // WORD], I32, name="w0_codes", align_bytes=LINE)
        w2_rows = w2.rearrange("(a p u j) n -> a u p j n", a=PASSES, u=2, j=2)
        w2_pairs = {
            (0, 0): keep.tile([P, 2, M], F32, name="w2_pair00", align_bytes=LINE),
            (0, 1): reuse.tile([P, 2, M], F32, name="w2_pair01", align_bytes=LINE, offset=FIELD0_SCALES_AT),
        }

        nc.sync.dma_start(w0_codes[:], w0_words.rearrange("a p c -> p a c").bitcast(I32))
        nc.sync.dma_start(offsets[:], offs)
        nc.sync.dma_start(staged[0:P:SPREAD, 0 : M // WORD], w0_scales.rearrange("a q n -> q a n").bitcast(I32))
        nc.sync.dma_start(b_cols[:], b.rearrange("(p c) -> p c", c=PACK))
        nc.sync.dma_start(
            scale_window[0:P:SPREAD, :], tab[:, K_PASS * T :].rearrange("a (q t) -> q a t", t=T).bitcast(I32)
        )
        for a in range(PASSES):
            nc.sync.dma_start(
                tab_words[a][:], tab[a, 0 : K_PASS * T].rearrange("(p w) -> p w", p=P).bitcast(I32)
            )
        nc.sync.dma_start(w2_pairs[0, 0][:], w2_rows[0, 0])

        warm_up = keep.tile([P, 1], F32, name="warm_up")
        nc.scalar.activation(warm_up[:], b_cols[:, 0:1], GELU)

        picked_words = [keep.tile([P, FIELDS * S], U32, name=f"picked_words{a}", align_bytes=LINE) for a in range(PASSES)]
        first_scales = reuse.tile([P, S], U8, name="first_scales", align_bytes=LINE, offset=FIELD0_SCALES_AT)
        later_scales = keep.tile([P, LATER], U8, name="later_scales", align_bytes=LINE)
        w2_codes = keep.tile([P, HALVES, PASSES, HALF], U32, name="w2_codes", align_bytes=LINE)
        w2_last_plane = keep.tile([P, M], U8, name="w2_last_plane", align_bytes=LINE)
        w2_scales = {
            (h, a): tile[:, h * HALF : (h + 1) * HALF]
            for h in range(HALVES)
            for a, tile in enumerate((weight_planes, w2_last_plane))
        }
        w2_bf16 = [keep.tile([P, M, PACK], BF16, name=f"w2_bf16_{a}", align_bytes=LINE) for a in range(PASSES)]

        def gather(dst, window, first_field, end_field):
            columns = slice(first_field * S // LIST_ROWS, end_field * S // LIST_ROWS)
            nc.vector.tensor_copy(dst[:], window.indirect(offsets[:, columns]))

        gather(later_scales, scale_window[:].bitcast(U8), 1, FIELDS)
        gather(first_scales, scale_window[:].bitcast(U8), 0, 1)
        nc.vector.tensor_copy(staged[:, M // WORD : PLANE // WORD], first_scales[:].bitcast(I32))
        for quad in MOVE_ORDER:
            nc.sync.dma_start(
                first_planes[QUAD * quad : QUAD * quad + ROWS, :, :].rearrange("p a n -> p (a n)"),
                staged[QUAD * quad : QUAD * (quad + 1) : SPREAD, :],
            )
        nc.sync.dma_start(w2_pairs[0, 1][:], w2_rows[0, 1])
        for quad in MOVE_ORDER:
            nc.gpsimd.dma_start(
                later_planes[QUAD * quad + 2 * ROWS : QUAD * quad + 3 * ROWS, :, :].rearrange("p a n -> p (a n)"),
                later_scales[QUAD * quad : QUAD * (quad + 1) : SPREAD, :].bitcast(I32),
            )
        for a in range(PASSES):
            gather(picked_words[a], tab_words[a][:].bitcast(U32), 0, FIELDS)

        bias_bank = psum.tile([P, PACK, P], F32, name="bias_bank")
        for c in range(PACK):
            nc.tensor.transpose(bias_bank[:, c, :], b_cols[:, c : c + 1].to_broadcast([P, P]), identity[:])
        bias = keep.tile([P, P, PACK], F32, name="bias")
        nc.scalar.copy(bias[:], bias_bank[:].rearrange("j c p -> j p c"))
        bias_row = bias[:].rearrange("j p c -> j (p c)")

        w2_pairs[1, 0] = reuse.tile([P, 2, M], F32, name="w2_pair10", align_bytes=LINE, offset=LATE_AT)
        nc.sync.dma_start(w2_pairs[1, 0][:], w2_rows[1, 0])
        last_run = reuse.tile([P, 2 * M], F32, name="last_run", align_bytes=LINE, offset=LATE_AT + 4 * KIB)
        last_rows = w2_rows[1, 1].rearrange("p j n -> p (j n)")
        for first, last in ((0, M + HALF), (M + HALF, 2 * M)):
            nc.sync.dma_start(last_run[:, first:last], last_rows[:, first:last])
        w2_pairs[1, 1] = last_run[:].rearrange("p (j n) -> p j n", j=2)
        w1_codes = {}
        w1_rows = w1_words.rearrange("a p n i -> p a (n i)").bitcast(I32)
        for a in range(PASSES):
            start = LATE_AT + (8 + a) * KIB
            w1_codes[0, a] = reuse.tile([P, HALF], I32, name=f"w1_first{a}", align_bytes=LINE, offset=start)[:]
            nc.sync.dma_start(w1_codes[0, a], w1_rows[:, a, 0:HALF])
        w1_second = reuse.tile([P, PASSES, HALF], I32, name="w1_second", align_bytes=LINE, offset=LATE_AT + 10 * KIB)
        nc.sync.dma_start(w1_second[:], w1_rows[:, :, HALF:M])
        for a in range(PASSES):
            w1_codes[1, a] = w1_second[:, a, :]

        def round_columns(copy, a, u, first, last):
            copy(
                w2_bf16[a][:, first:last, 2 * u : 2 * u + 2].rearrange("p (c i) j -> p c j i", i=4),
                w2_pairs[a, u][:, :, first:last].rearrange("p j (c i) -> p c j i", i=4),
            )

        def quantize_halves(a):
            for h in range(HALVES):
                nc.vector.quantize_mx(
                    out=w2_codes[:, h, a, :].bitcast(FP8X4),
                    scales=w2_scales[h, a],
                    in_=w2_bf16[a][:, h * HALF : (h + 1) * HALF, :].rearrange("p n j -> p (n j)"),
                )

        def round_pair(a, u):
            split = M - SCALAR_COLUMNS[a][u]
            round_columns(nc.vector.tensor_copy, a, u, 0, min(split, HALF))
            round_columns(nc.scalar.copy, a, u, split, M)
            if split > HALF:
                round_columns(nc.vector.tensor_copy, a, u, HALF, split)

        round_pair(0, 0)
        round_pair(0, 1)
        quantize_halves(0)
        round_pair(1, 0)
        round_columns(nc.scalar.copy, 1, 1, 0, FIRST_SHARE)
        round_columns(nc.vector.tensor_copy, 1, 1, FIRST_SHARE, HALF - SEAM)
        round_columns(nc.scalar.copy, 1, 1, M - SCALAR_COLUMNS[1][1], M)
        round_columns(nc.vector.tensor_copy, 1, 1, HALF - SEAM, HALF + SEAM)
        round_columns(nc.vector.tensor_copy, 1, 1, HALF + SEAM, M - SCALAR_COLUMNS[1][1])
        quantize_halves(1)

        first_bytes = first_planes[:].bitcast(U8)
        later_bytes = later_planes[2 * ROWS : P, :, :].bitcast(U8)
        w0_bytes = w0_codes[:].bitcast(U8)
        half_sums = [
            [(0, 0, HALF), (1, 0, HALF)],
            [(0, HALF, HALF), (1, HALF, P), (1, HALF + P, P)],
        ]
        sums = half_sums[0] + half_sums[1]
        acc = {s: psum.tile([P, s[2]], F32, name=f"acc{s[0]}_{s[1]}") for s in sums}

        def table_pass(s, f, a, cols, rhs, rhs_scale, start, stop):
            token = f * S + s[0] * P
            if f == 0:
                token_scales = first_bytes[:, a, M + token : M + token + P]
            else:
                token_scales = later_bytes[:, a, token - S : token - S + P]
            nc.tensor.matmul_mx(
                out=acc[s][:, cols],
                lhsT=picked_words[a][:, token : token + P].bitcast(FP8X4),
                lhsT_scale=token_scales,
                rhs=rhs,
                rhs_scale=rhs_scale,
                start=start,
                stop=stop,
            )

        def w0_passes(s, a):
            for c0 in range(0, s[2], P):
                n0 = s[1] + c0
                table_pass(
                    s, 0, a, slice(c0, c0 + P), w0_bytes[:, a, 2 * n0 : 2 * (n0 + P)].bitcast(FP4X4),
                    first_bytes[:, a, n0 : n0 + P], a == 0 and c0 == 0, False,
                )

        def w1_pass(s, a):
            h, c0 = divmod(s[1], HALF)
            table_pass(
                s, 1, a, slice(0, s[2]), w1_codes[h, a][:, c0 : c0 + s[2]].bitcast(FP8X4),
                weight_planes[ROWS * (1 + a) : P, s[1] : s[1] + s[2]], False, False,
            )

        def w2_pass(s, a):
            h, c0 = divmod(s[1], HALF)
            table_pass(
                s, 2, a, slice(0, s[2]), w2_codes[:, h, a, c0 : c0 + s[2]].bitcast(FP8X4),
                w2_scales[h, a][:, c0 : c0 + s[2]], False, a == PASSES - 1,
            )

        for a in range(PASSES):
            for s in sums:
                w0_passes(s, a)
        for s in sums:
            w2_pass(s, 0)
        for a in range(PASSES):
            for s in half_sums[0]:
                w1_pass(s, a)
        for s in half_sums[0]:
            w2_pass(s, 1)
        for s in half_sums[1]:
            w1_pass(s, 0)
            w1_pass(s, 1)
            w2_pass(s, 1)

        out_view = out.rearrange("(tt p) n -> p tt n", p=P)
        summed = [keep.tile([P, M], F32, name=f"summed{tt}") for tt in range(TOKEN_TILES)]
        result = [keep.tile([P, M], F32, name=f"result{tt}", align_bytes=LINE) for tt in range(TOKEN_TILES)]
        for s in sums:
            tt, first, width = s
            for n0 in range(first, first + width, P):
                cols = slice(n0, n0 + P)
                nc.vector.tensor_tensor(
                    summed[tt][:, cols], acc[s][:, n0 - first : n0 - first + P], bias_row[:, cols], mybir.AluOpType.add
                )
                nc.scalar.activation(result[tt][:, cols], summed[tt][:, cols], GELU)
                if s == sums[0]:
                    nc.sync.dma_start(out_view[:, tt, cols], result[tt][:, cols])
                elif (n0 + P) % HALF == 0:
                    half = slice(n0 + P - HALF, n0 + P)
                    nc.sync.dma_start(out_view[:, tt, half], result[tt][:, half])
